import numpy as np
import ml_dtypes


def mxq(x, axis, fmt="e4m3"):
    dtype, down = {"e4m3": (ml_dtypes.float8_e4m3fn, 7), "e5m2": (ml_dtypes.float8_e5m2, 14)}[fmt]
    v = np.moveaxis(np.asarray(x, np.float32).astype(ml_dtypes.bfloat16).astype(np.float64), axis, -1)
    blocks = v.reshape(v.shape[:-1] + (-1, 32))
    amax = np.abs(blocks).max(-1, keepdims=True)
    byte = np.maximum(np.where(amax > 0, np.frexp(amax)[1] - 1 + 127, 0) - down, 1)
    scale = np.exp2(byte - 127.0)
    codes = (blocks / scale).astype(np.float32).astype(dtype).astype(np.float64)
    return np.moveaxis((codes * scale).reshape(v.shape), -1, axis)


WIDE = False


def mx_kscale(k):
    if not WIDE:
        return np.ones(k)
    levels = np.array([10, -10, 5, -5, 0])
    if k % 512:
        return np.exp2(np.random.permutation(np.resize(levels, k // 32))).repeat(32)
    a = np.empty((k // 512, 16))
    for p in range(k // 512):
        a[p, :8] = np.random.permutation(np.resize(levels, 8))
        for g in range(8):
            far = levels[np.abs(levels - a[p, g]) >= 10]
            a[p, g + 8] = far[np.random.randint(len(far))]
    return np.exp2(a.ravel()).repeat(32)


def f64(x):
    return np.asarray(x).astype(np.float64)


def striped(idx):
    return np.tile(idx.reshape(-1, 16).T, (8, 1)).astype(np.uint16)


def unstriped(offs):
    return offs[:16].T.reshape(-1).astype(np.int64)


def striped8(idx):
    return np.concatenate([x.reshape(-1, 16).T for x in idx]).astype(np.uint16)


def runs(offs, k):
    lists = np.stack([offs[16 * r : 16 * r + 16].T.reshape(-1) for r in range(8)]).astype(np.int64)
    return lists[np.arange(k) % 512 // 64]


def pack_weight(w):
    k, n = w.shape
    w = f64(np.asarray(w, np.float32).astype(ml_dtypes.bfloat16)).reshape(k // 32, 32, n)
    amax = np.abs(w).max(1)
    byte = np.clip(np.where(amax > 0, np.frexp(amax)[1] - 1 + 127 - 7, 1), 1, 254)
    scaled = (w * np.exp2(127.0 - byte)[:, None, :]).reshape(k, n).astype(np.float32)
    words = np.ascontiguousarray(scaled.reshape(k // 512, 128, 4, n).transpose(0, 1, 3, 2)).astype(ml_dtypes.float8_e4m3fn).view(np.uint8)
    return words, np.ascontiguousarray(byte.astype(np.uint8).reshape(k // 512, 16, n))


def unpack_weight(words, scales):
    g, p, n, _ = words.shape
    vals = np.ascontiguousarray(words).view(ml_dtypes.float8_e4m3fn).astype(np.float64) * np.repeat(np.exp2(scales.astype(np.float64) - 127.0), 8, axis=1)[..., None]
    return vals.transpose(0, 1, 3, 2).reshape(g * 512, n)


def relu(v):
    return np.maximum(v, 0.0)


K, T, S, N, H = 512, 2048, 512, 512, 512


def setup_inputs():
    n = np.random.standard_normal
    s = mx_kscale(K)[:, None]
    u = mx_kscale(H)
    packed_xT = pack_weight(n((K, T)) * s)
    return {
        "x_words": packed_xT[0],
        "x_scales": packed_xT[1],
        "w1": (n((K, H)) / np.sqrt(K) / s).astype(np.float32),
        "gn": (np.random.uniform(0.5, 1.5, (H, 1)) * u[:, None]).astype(np.float32),
        "w2": (n((H, N)) / np.sqrt(H) / u[:, None]).astype(np.float32),
        "offs": striped(np.random.permutation(T)[:S]),
        "east": striped8(np.stack([np.random.permutation(S) for _ in range(8)])),
        "west": striped8(np.stack([np.random.permutation(S) for _ in range(8)])),
    }


def reference(x_words, x_scales, w1, gn, w2, offs, east, west):
    xq = unpack_weight(x_words, x_scales)[:, unstriped(offs)]
    y = mxq(f64(w1), 0, "e4m3").T @ xq
    a = y - (y[np.arange(H)[:, None], runs(west, H)])
    b = y[np.arange(H)[:, None], runs(east, H)] - y
    mn = np.minimum(a, b)
    mx = np.maximum(a, b)
    z = f64(gn) * (y + 0.5 * (relu(mn) + mx - relu(mx)))
    return mxq(f64(w2), 0, "e4m3").T @ mxq(z, 0, "e4m3")

@@ -1,0 +1,195 @@
+from contextlib import ExitStack
+
+import concourse.mybir as mybir
+
+K, T, S, N, H = 512, 2048, 512, 512, 512
+FLOPS = 2 * K * H * S + 2 * H * N * S
+
+F32 = mybir.dt.float32
+BF16 = mybir.dt.bfloat16
+I32 = mybir.dt.int32
+U32 = mybir.dt.uint32
+U16 = mybir.dt.uint16
+U8 = mybir.dt.uint8
+FP8X4 = mybir.dt.float8_e4m3fn_x4
+ALU = mybir.AluOpType
+COPY = mybir.ActivationFunctionType.Copy
+
+P = 128
+PACK = 4
+HALF = S // 2
+CHUNKS = [(0, 256), (256, 128), (384, 128)]
+M_VECTOR = 96
+B_TAGS = {(2, 0): "z_bf0", (2, 3): "z_bf1"}
+
+
+def tile_picked_minmod_none_p_kernel(tc, x_words, x_scales, w1, gn, w2, offs, east, west, out):
+    nc = tc.nc
+    with ExitStack() as ctx:
+        sb = ctx.enter_context(tc.tile_pool(name="sb", bufs=1))
+        psum = ctx.enter_context(tc.psum_pool(name="psum", bufs=1))
+
+        offs_sb = sb.tile([P, S // 16], U16, name="offs_sb")
+        east_sb = sb.tile([P, S // 16], U16, name="east_sb")
+        west_sb = sb.tile([P, S // 16], U16, name="west_sb")
+        xw = sb.tile([P, T], U32, name="xw", align_bytes=64)
+        xs = sb.tile([P, T], U8, name="xs", tag="xs", align_bytes=64)
+        w1_raw = sb.tile([P, PACK, H], F32, name="w1_raw", align_bytes=64)
+        w2_raw = sb.tile([P, PACK, N], F32, name="w2_raw", align_bytes=64)
+        gn_sb = sb.tile([P, PACK], F32, name="gn_sb")
+        g_pos = sb.tile([P, PACK], F32, name="g_pos")
+        g_neg = sb.tile([P, PACK], F32, name="g_neg")
+
+        nc.vector.memset(xs[:].bitcast(I32), 0)
+        nc.sync.dma_start(offs_sb[:], offs)
+        nc.sync.dma_start(w1_raw[:], w1.rearrange("(p j) c -> p j c", j=PACK))
+        for q in range(4):
+            nc.scalar.dma_start(xs[32 * q : 32 * q + 4, :].bitcast(I32), x_scales[0, 4 * q : 4 * q + 4, :].bitcast(I32))
+        nc.scalar.dma_start(gn_sb[:], gn.rearrange("(p t) o -> p (t o)", t=PACK))
+        nc.sync.dma_start(xw[:].bitcast(I32), x_words[0].rearrange("p n t -> p (n t)").bitcast(I32))
+        nc.sync.dma_start(east_sb[:], east)
+        nc.sync.dma_start(west_sb[:], west)
+        nc.sync.dma_start(w2_raw[:], w2.rearrange("(p j) c -> p j c", j=PACK))
+
+        nc.scalar.activation(g_pos[:], gn_sb[:], COPY, scale=0.5)
+        nc.scalar.activation(g_neg[:], gn_sb[:], COPY, scale=-0.5)
+
+        xg_scales = sb.tile([P, S], U8, name="xg_scales", align_bytes=64)
+        nc.vector.tensor_copy(xg_scales[:], xs[:].indirect(offs_sb[:]))
+
+        w1_bf = sb.tile([P, PACK * H], BF16, name="w1_bf", align_bytes=64)
+        w1_dst = w1_bf[:].rearrange("p (t m j) -> p m t j", t=PACK, j=PACK)
+        w1_src = w1_raw[:].rearrange("p j (m t) -> p m t j", t=PACK)
+        nc.vector.tensor_copy(w1_dst[:, :M_VECTOR], w1_src[:, :M_VECTOR])
+        nc.scalar.copy(w1_dst[:, M_VECTOR:], w1_src[:, M_VECTOR:])
+        w1_codes = sb.tile([P, H], U32, name="w1_codes", tag="w1_codes", align_bytes=64)
+        w1_scales = sb.tile([P, H], U8, name="w1_scales", align_bytes=64)
+        nc.vector.quantize_mx(out=w1_codes[:].bitcast(FP8X4), scales=w1_scales[:], in_=w1_bf[:])
+
+        xg = [sb.tile([P, HALF], U32, name=f"xg{h}", tag=("xs", "xg1")[h], align_bytes=64) for h in range(2)]
+        for h in range(2):
+            nc.vector.tensor_copy(xg[h][:], xw[:].indirect(offs_sb[:, 16 * h : 16 * h + 16]))
+
+        u = [sb.tile([P, S], F32, name=f"u{t}", align_bytes=64) for t in range(PACK)]
+        v = [sb.tile([P, S], F32, name=f"v{t}", align_bytes=64) for t in range(PACK)]
+
+        def first_product(acc, t, h):
+            nc.tensor.matmul_mx(
+                out=acc,
+                lhsT=w1_codes[:, t * P : (t + 1) * P].bitcast(FP8X4),
+                lhsT_scale=w1_scales[:, t * P : (t + 1) * P],
+                rhs=xg[h][:].bitcast(FP8X4),
+                rhs_scale=xg_scales[:, h * HALF : (h + 1) * HALF],
+                start=True,
+                stop=True,
+            )
+
+        def leave(t, cols, acc):
+            nc.scalar.activation(u[t][:, cols], acc, COPY, scale=g_pos[:, t : t + 1])
+            nc.scalar.activation(v[t][:, cols], acc, COPY, scale=g_neg[:, t : t + 1])
+
+        for h in range(2):
+            acc = psum.tile([P, HALF], F32, name=f"y0{h}", tag=f"bank{h}")
+            first_product(acc[:], 0, h)
+            leave(0, slice(h * HALF, (h + 1) * HALF), acc[:])
+        for t in range(1, PACK):
+            acc = psum.tile([P, S], F32, name=f"y{t}", tag=f"bank{t + 1}")
+            for h in range(2):
+                first_product(acc[:, h * HALF : (h + 1) * HALF], t, h)
+            leave(t, slice(0, S), acc[:])
+
+        w2_bf = sb.tile([P, PACK * N], BF16, name="w2_bf", tag="w1_codes", align_bytes=64)
+        w2_dst = w2_bf[:].rearrange("p (c i j) -> p c j i", i=4, j=PACK)
+        w2_src = w2_raw[:].rearrange("p j (c i) -> p c j i", i=4)
+        for part in range(4):
+            nc.scalar.copy(w2_dst[:, 32 * part : 32 * part + 32], w2_src[:, 32 * part : 32 * part + 32])
+        w2_codes = sb.tile([P, N], U32, name="w2_codes", align_bytes=64)
+        w2_scales = sb.tile([P, N], U8, name="w2_scales", align_bytes=64)
+
+        units = [(c, t) for c in range(len(CHUNKS)) for t in range(PACK)]
+        a = {}
+        b = {}
+        low = {}
+        mm = {}
+        z = [sb.tile([P, PACK, width], F32, name=f"z{c}", align_bytes=64) for c, (start, width) in enumerate(CHUNKS)]
+
+        def cols_of(c):
+            return slice(CHUNKS[c][0], CHUNKS[c][0] + CHUNKS[c][1])
+
+        def list_cols(c):
+            return slice(CHUNKS[c][0] // 16, (CHUNKS[c][0] + CHUNKS[c][1]) // 16)
+
+        def gather_east(c, t):
+            b[c, t] = sb.tile([P, CHUNKS[c][1]], F32, name=f"b{c}{t}", tag=B_TAGS.get((c, t), f"b{(4 * c + t) % 3}"), align_bytes=64)
+            nc.vector.tensor_tensor(b[c, t][:], u[t][:].indirect(east_sb[:, list_cols(c)]), v[t][:, cols_of(c)], ALU.add)
+
+        def gather_west(c, t):
+            a[c, t] = sb.tile([P, CHUNKS[c][1]], F32, name=f"a{c}{t}", tag=f"a{(4 * c + t) % 3}", align_bytes=64)
+            nc.vector.tensor_tensor(a[c, t][:], v[t][:].indirect(west_sb[:, list_cols(c)]), u[t][:, cols_of(c)], ALU.add)
+
+        def clamp_low(c, t):
+            low[c, t] = sb.tile([P, CHUNKS[c][1]], F32, name=f"low{c}{t}", align_bytes=64)
+            nc.vector.scalar_tensor_tensor(low[c, t][:], b[c, t][:], 0.0, a[c, t][:], ALU.min, ALU.max)
+
+        def clamp_high(c, t):
+            mm[c, t] = sb.tile([P, CHUNKS[c][1]], F32, name=f"mm{c}{t}", align_bytes=64)
+            nc.vector.scalar_tensor_tensor(mm[c, t][:], b[c, t][:], 0.0, low[c, t][:], ALU.max, ALU.min)
+
+        def add_centre(c, t):
+            nc.vector.scalar_tensor_tensor(z[c][:, t, :], u[t][:, cols_of(c)], 2.0, mm[c, t][:], ALU.mult, ALU.add)
+
+        z_bf = {}
+
+        def interleave(c):
+            width = CHUNKS[c][1]
+            z_bf[c] = sb.tile([P, PACK * width], BF16, name=f"z_bf{c}", tag=f"z_bf{c}", align_bytes=64)
+            nc.scalar.copy(
+                z_bf[c][:].rearrange("p (c i t) -> p c t i", i=4, t=PACK),
+                z[c][:].rearrange("p t (c i) -> p c t i", i=4),
+            )
+
+        def second_product(c):
+            width = CHUNKS[c][1]
+            codes = sb.tile([P, width], U32, name=f"z_codes{c}", align_bytes=64)
+            scales = sb.tile([P, width], U8, name=f"z_scales{c}", align_bytes=64)
+            nc.vector.quantize_mx(out=codes[:].bitcast(FP8X4), scales=scales[:], in_=z_bf[c][:])
+            per_bank = 2
+            for half in range(2):
+                acc = psum.tile([P, per_bank, width], F32, name=f"o{c}{half}", tag=f"bank{5 + (2 * c + half) % 3}")
+                res = sb.tile([P, per_bank, width], F32, name=f"res{c}{half}", align_bytes=64)
+                for g in range(per_bank):
+                    rows = slice((half * per_bank + g) * P, (half * per_bank + g + 1) * P)
+                    nc.tensor.matmul_mx(
+                        out=acc[:, g, :],
+                        lhsT=w2_codes[:, rows].bitcast(FP8X4),
+                        lhsT_scale=w2_scales[:, rows],
+                        rhs=codes[:].bitcast(FP8X4),
+                        rhs_scale=scales[:],
+                        start=True,
+                        stop=True,
+                    )
+                if c == len(CHUNKS) - 1 and half == 1:
+                    nc.vector.tensor_copy(res[:], acc[:])
+                else:
+                    nc.scalar.copy(res[:], acc[:])
+                dst = out[half * per_bank * P : (half + 1) * per_bank * P, cols_of(c)].rearrange("(g p) n -> p g n", p=P)
+                nc.sync.dma_start(dst, res[:])
+
+        for i in range(len(units) + 2):
+            if i < len(units):
+                gather_east(*units[i])
+            if 1 <= i <= len(units):
+                clamp_low(*units[i - 1])
+            if i < len(units):
+                gather_west(*units[i])
+            if i >= 2:
+                add_centre(*units[i - 2])
+                if units[i - 2][1] == PACK - 1:
+                    interleave(units[i - 2][0])
+            if 1 <= i <= len(units):
+                clamp_high(*units[i - 1])
+            if i == 5:
+                nc.vector.quantize_mx(out=w2_codes[:].bitcast(FP8X4), scales=w2_scales[:], in_=w2_bf[:])
+            if i in (7, 10):
+                second_product((i - 7) // 3)
+        second_product(len(CHUNKS) - 1)

@@ -1,6 +1,7 @@
 from contextlib import ExitStack
 
 import concourse.mybir as mybir
+from concourse.masks import make_identity
 
 K, T, S, N, H = 512, 2048, 512, 512, 512
 FLOPS = 2 * K * H * S + 2 * H * N * S
@@ -19,8 +20,7 @@ P = 128
 PACK = 4
 HALF = S // 2
 CHUNKS = [(0, 256), (256, 128), (384, 128)]
-M_VECTOR = 96
-B_TAGS = {(2, 0): "z_bf0", (2, 3): "z_bf1"}
+M_VECTOR = 64
 
 
 def tile_picked_minmod_none_p_kernel(tc, x_words, x_scales, w1, gn, w2, offs, east, west, out):
@@ -34,41 +34,45 @@ def tile_picked_minmod_none_p_kernel(tc, x_words, x_scales, w1, gn, w2, offs, ea
         west_sb = sb.tile([P, S // 16], U16, name="west_sb")
         xw = sb.tile([P, T], U32, name="xw", align_bytes=64)
         xs = sb.tile([P, T], U8, name="xs", tag="xs", align_bytes=64)
-        w1_raw = sb.tile([P, PACK, H], F32, name="w1_raw", align_bytes=64)
-        w2_raw = sb.tile([P, PACK, N], F32, name="w2_raw", align_bytes=64)
+        w1_raw = sb.tile([P, PACK, H], F32, name="w1_raw", tag="w_raw", align_bytes=64)
         gn_sb = sb.tile([P, PACK], F32, name="gn_sb")
         g_pos = sb.tile([P, PACK], F32, name="g_pos")
         g_neg = sb.tile([P, PACK], F32, name="g_neg")
+        ident = sb.tile([P, P], F32, name="ident", align_bytes=64)
 
         nc.vector.memset(xs[:].bitcast(I32), 0)
-        nc.sync.dma_start(offs_sb[:], offs)
+        nc.scalar.dma_start(gn_sb[:], gn.rearrange("(p t) o -> p (t o)", t=PACK))
         nc.sync.dma_start(w1_raw[:], w1.rearrange("(p j) c -> p j c", j=PACK))
+        nc.sync.dma_start(offs_sb[:], offs)
         for q in range(4):
             nc.scalar.dma_start(xs[32 * q : 32 * q + 4, :].bitcast(I32), x_scales[0, 4 * q : 4 * q + 4, :].bitcast(I32))
-        nc.scalar.dma_start(gn_sb[:], gn.rearrange("(p t) o -> p (t o)", t=PACK))
         nc.sync.dma_start(xw[:].bitcast(I32), x_words[0].rearrange("p n t -> p (n t)").bitcast(I32))
         nc.sync.dma_start(east_sb[:], east)
         nc.sync.dma_start(west_sb[:], west)
-        nc.sync.dma_start(w2_raw[:], w2.rearrange("(p j) c -> p j c", j=PACK))
+        make_identity(nc, ident[:])
 
         nc.scalar.activation(g_pos[:], gn_sb[:], COPY, scale=0.5)
         nc.scalar.activation(g_neg[:], gn_sb[:], COPY, scale=-0.5)
-
-        xg_scales = sb.tile([P, S], U8, name="xg_scales", align_bytes=64)
-        nc.vector.tensor_copy(xg_scales[:], xs[:].indirect(offs_sb[:]))
 
         w1_bf = sb.tile([P, PACK * H], BF16, name="w1_bf", align_bytes=64)
         w1_dst = w1_bf[:].rearrange("p (t m j) -> p m t j", t=PACK, j=PACK)
         w1_src = w1_raw[:].rearrange("p j (m t) -> p m t j", t=PACK)
         nc.vector.tensor_copy(w1_dst[:, :M_VECTOR], w1_src[:, :M_VECTOR])
         nc.scalar.copy(w1_dst[:, M_VECTOR:], w1_src[:, M_VECTOR:])
+
+        w2_raw = sb.tile([P, PACK, N], F32, name="w2_raw", tag="w_raw", align_bytes=64)
+        nc.sync.dma_start(w2_raw[:], w2.rearrange("(p j) c -> p j c", j=PACK))
+
+        xg_scales = sb.tile([P, S], U8, name="xg_scales", align_bytes=64)
+        nc.vector.tensor_copy(xg_scales[:], xs[:].indirect(offs_sb[:]))
+
         w1_codes = sb.tile([P, H], U32, name="w1_codes", tag="w1_codes", align_bytes=64)
         w1_scales = sb.tile([P, H], U8, name="w1_scales", align_bytes=64)
         nc.vector.quantize_mx(out=w1_codes[:].bitcast(FP8X4), scales=w1_scales[:], in_=w1_bf[:])
 
-        xg = [sb.tile([P, HALF], U32, name=f"xg{h}", tag=("xs", "xg1")[h], align_bytes=64) for h in range(2)]
+        xg = sb.tile([P, S], U32, name="xg", tag="xs", align_bytes=64)
         for h in range(2):
-            nc.vector.tensor_copy(xg[h][:], xw[:].indirect(offs_sb[:, 16 * h : 16 * h + 16]))
+            nc.vector.tensor_copy(xg[:, h * HALF : (h + 1) * HALF], xw[:].indirect(offs_sb[:, 16 * h : 16 * h + 16]))
 
         u = [sb.tile([P, S], F32, name=f"u{t}", align_bytes=64) for t in range(PACK)]
         v = [sb.tile([P, S], F32, name=f"v{t}", align_bytes=64) for t in range(PACK)]
@@ -78,7 +82,7 @@ def tile_picked_minmod_none_p_kernel(tc, x_words, x_scales, w1, gn, w2, offs, ea
                 out=acc,
                 lhsT=w1_codes[:, t * P : (t + 1) * P].bitcast(FP8X4),
                 lhsT_scale=w1_scales[:, t * P : (t + 1) * P],
-                rhs=xg[h][:].bitcast(FP8X4),
+                rhs=xg[:, h * HALF : (h + 1) * HALF].bitcast(FP8X4),
                 rhs_scale=xg_scales[:, h * HALF : (h + 1) * HALF],
                 start=True,
                 stop=True,
@@ -91,7 +95,12 @@ def tile_picked_minmod_none_p_kernel(tc, x_words, x_scales, w1, gn, w2, offs, ea
         for h in range(2):
             acc = psum.tile([P, HALF], F32, name=f"y0{h}", tag=f"bank{h}")
             first_product(acc[:], 0, h)
-            leave(0, slice(h * HALF, (h + 1) * HALF), acc[:])
+            cols = slice(h * HALF, (h + 1) * HALF)
+            if h == 0:
+                nc.scalar.activation(u[0][:, cols], acc[:], COPY, scale=g_pos[:, 0:1])
+            else:
+                nc.vector.tensor_scalar(u[0][:, cols], acc[:], g_pos[:, 0:1], None, ALU.mult)
+            nc.scalar.activation(v[0][:, cols], acc[:], COPY, scale=g_neg[:, 0:1])
         for t in range(1, PACK):
             acc = psum.tile([P, S], F32, name=f"y{t}", tag=f"bank{t + 1}")
             for h in range(2):
@@ -101,64 +110,99 @@ def tile_picked_minmod_none_p_kernel(tc, x_words, x_scales, w1, gn, w2, offs, ea
         w2_bf = sb.tile([P, PACK * N], BF16, name="w2_bf", tag="w1_codes", align_bytes=64)
         w2_dst = w2_bf[:].rearrange("p (c i j) -> p c j i", i=4, j=PACK)
         w2_src = w2_raw[:].rearrange("p j (c i) -> p c j i", i=4)
-        for part in range(4):
-            nc.scalar.copy(w2_dst[:, 32 * part : 32 * part + 32], w2_src[:, 32 * part : 32 * part + 32])
+        for part in range(2):
+            nc.scalar.copy(w2_dst[:, 64 * part : 64 * part + 64], w2_src[:, 64 * part : 64 * part + 64])
         w2_codes = sb.tile([P, N], U32, name="w2_codes", align_bytes=64)
         w2_scales = sb.tile([P, N], U8, name="w2_scales", align_bytes=64)
 
-        units = [(c, t) for c in range(len(CHUNKS)) for t in range(PACK)]
         a = {}
         b = {}
         low = {}
-        mm = {}
-        z = [sb.tile([P, PACK, width], F32, name=f"z{c}", align_bytes=64) for c, (start, width) in enumerate(CHUNKS)]
+        slope = {}
 
-        def cols_of(c):
+        def planes(c, t0, t1):
+            return slice(t0 * CHUNKS[c][1], t1 * CHUNKS[c][1])
+
+        def cells(c):
             return slice(CHUNKS[c][0], CHUNKS[c][0] + CHUNKS[c][1])
 
         def list_cols(c):
             return slice(CHUNKS[c][0] // 16, (CHUNKS[c][0] + CHUNKS[c][1]) // 16)
 
-        def gather_east(c, t):
-            b[c, t] = sb.tile([P, CHUNKS[c][1]], F32, name=f"b{c}{t}", tag=B_TAGS.get((c, t), f"b{(4 * c + t) % 3}"), align_bytes=64)
-            nc.vector.tensor_tensor(b[c, t][:], u[t][:].indirect(east_sb[:, list_cols(c)]), v[t][:, cols_of(c)], ALU.add)
+        def gather_east(c, t, tag=None):
+            if t == 0:
+                b[c] = sb.tile([P, PACK * CHUNKS[c][1]], F32, name=f"b{c}", tag=tag or f"b{c}", align_bytes=64)
+            nc.vector.tensor_tensor(b[c][:, planes(c, t, t + 1)], u[t][:].indirect(east_sb[:, list_cols(c)]), v[t][:, cells(c)], ALU.add)
 
-        def gather_west(c, t):
-            a[c, t] = sb.tile([P, CHUNKS[c][1]], F32, name=f"a{c}{t}", tag=f"a{(4 * c + t) % 3}", align_bytes=64)
-            nc.vector.tensor_tensor(a[c, t][:], v[t][:].indirect(west_sb[:, list_cols(c)]), u[t][:, cols_of(c)], ALU.add)
+        def gather_west(c, t, tag=None):
+            if t == 0:
+                a[c] = sb.tile([P, PACK * CHUNKS[c][1]], F32, name=f"a{c}", tag=tag or f"a{c}", align_bytes=64)
+            nc.vector.tensor_tensor(a[c][:, planes(c, t, t + 1)], v[t][:].indirect(west_sb[:, list_cols(c)]), u[t][:, cells(c)], ALU.add)
 
-        def clamp_low(c, t):
-            low[c, t] = sb.tile([P, CHUNKS[c][1]], F32, name=f"low{c}{t}", align_bytes=64)
-            nc.vector.scalar_tensor_tensor(low[c, t][:], b[c, t][:], 0.0, a[c, t][:], ALU.min, ALU.max)
+        def clamp_low(c, t0, t1, tag=None):
+            name = f"low{c}{t0}"
+            low[c, t0] = sb.tile([P, (t1 - t0) * CHUNKS[c][1]], F32, name=name, tag=tag or name, align_bytes=64)
+            nc.vector.scalar_tensor_tensor(low[c, t0][:], b[c][:, planes(c, t0, t1)], 0.0, a[c][:, planes(c, t0, t1)], ALU.min, ALU.max)
 
-        def clamp_high(c, t):
-            mm[c, t] = sb.tile([P, CHUNKS[c][1]], F32, name=f"mm{c}{t}", align_bytes=64)
-            nc.vector.scalar_tensor_tensor(mm[c, t][:], b[c, t][:], 0.0, low[c, t][:], ALU.max, ALU.min)
+        def clamp_high(c, t0, t1, tag=None):
+            name = f"slope{c}{t0}"
+            width = CHUNKS[c][1]
+            tile = sb.tile([P, (t1 - t0) * width], F32, name=name, tag=tag or name, align_bytes=64)
+            nc.vector.scalar_tensor_tensor(tile[:], b[c][:, planes(c, t0, t1)], 0.0, low[c, t0][:], ALU.max, ALU.min)
+            for t in range(t0, t1):
+                for i in range(width // P):
+                    slope[CHUNKS[c][0] // P + i, t] = tile[:, (t - t0) * width + i * P : (t - t0) * width + (i + 1) * P]
 
-        def add_centre(c, t):
-            nc.vector.scalar_tensor_tensor(z[c][:, t, :], u[t][:, cols_of(c)], 2.0, mm[c, t][:], ALU.mult, ALU.add)
-
+        zt = {}
         z_bf = {}
 
-        def interleave(c):
-            width = CHUNKS[c][1]
-            z_bf[c] = sb.tile([P, PACK * width], BF16, name=f"z_bf{c}", tag=f"z_bf{c}", align_bytes=64)
+        def open_sum(r):
+            zt[r] = psum.tile([P, PACK, P], F32, name=f"zt{r}", tag=f"bank{(5, 6, 0, 1)[r]}")
+            for t in range(PACK):
+                for rep in range(2):
+                    nc.tensor.matmul(zt[r][:, t, :], u[t][:, r * P : (r + 1) * P], ident[:], start=(t == 0 and rep == 0), stop=False, is_transpose=True)
+
+        def add_slope(r, t0, t1):
+            for t in range(t0, t1):
+                nc.tensor.matmul(zt[r][:, t, :], slope[r, t], ident[:], start=False, stop=(t == PACK - 1), is_transpose=True)
+
+        def turn_back(r):
+            rounded = sb.tile([P, PACK * P], BF16, name=f"rounded{r}", align_bytes=64)
             nc.scalar.copy(
-                z_bf[c][:].rearrange("p (c i t) -> p c t i", i=4, t=PACK),
-                z[c][:].rearrange("p t (c i) -> p c t i", i=4),
+                rounded[:].rearrange("c (e p k) -> c e p k", e=2, k=2),
+                zt[r][:].rearrange("c (e k) p -> c e p k", k=2),
+            )
+            pairs = psum.tile([P, 2, P], F32, name=f"pairs{r}", tag=f"bank{(7, 2)[r % 2]}")
+            for e in range(2):
+                nc.tensor.transpose(pairs[:, e, :], rounded[:].bitcast(F32)[:, e * P : (e + 1) * P], ident[:])
+            z_bf[r] = sb.tile([P, PACK * P], BF16, name=f"z_bf{r}", tag=f"z_bf{r}", align_bytes=64)
+            dst = z_bf[r][:].bitcast(F32).rearrange("p (c e) -> p c e", e=2)
+            src = pairs[:].rearrange("p e c -> p c e")
+            nc.scalar.copy(dst, src)
+
+        z_last = sb.tile([P, PACK, P], BF16, name="z_last", align_bytes=64)
+
+        def add_centre(t):
+            nc.vector.scalar_tensor_tensor(z_last[:, t, :], u[t][:, 3 * P : 4 * P], 2.0, slope[3, t], ALU.mult, ALU.add)
+
+        def interleave_last():
+            z_bf[3] = sb.tile([P, PACK * P], BF16, name="z_bf3", align_bytes=64)
+            nc.vector.tensor_copy(
+                z_bf[3][:].rearrange("p (c i t) -> p c t i", i=4, t=PACK),
+                z_last[:].rearrange("p t (c i) -> p c t i", i=4),
             )
 
-        def second_product(c):
-            width = CHUNKS[c][1]
-            codes = sb.tile([P, width], U32, name=f"z_codes{c}", align_bytes=64)
-            scales = sb.tile([P, width], U8, name=f"z_scales{c}", align_bytes=64)
-            nc.vector.quantize_mx(out=codes[:].bitcast(FP8X4), scales=scales[:], in_=z_bf[c][:])
-            per_bank = 2
-            for half in range(2):
-                acc = psum.tile([P, per_bank, width], F32, name=f"o{c}{half}", tag=f"bank{5 + (2 * c + half) % 3}")
-                res = sb.tile([P, per_bank, width], F32, name=f"res{c}{half}", align_bytes=64)
-                for g in range(per_bank):
-                    rows = slice((half * per_bank + g) * P, (half * per_bank + g + 1) * P)
+        def second_product(r):
+            codes = sb.tile([P, P], U32, name=f"z_codes{r}", align_bytes=64)
+            scales = sb.tile([P, P], U8, name=f"z_scales{r}", align_bytes=64)
+            nc.vector.quantize_mx(out=codes[:].bitcast(FP8X4), scales=scales[:], in_=z_bf[r][:])
+            parts = 2 if r == 3 else 1
+            per = PACK // parts
+            for part in range(parts):
+                acc = psum.tile([P, per, P], F32, name=f"o{r}{part}", tag=f"bank{(3, 4, 5, 6, 1)[r + part]}")
+                res = sb.tile([P, per, P], F32, name=f"res{r}{part}", align_bytes=64)
+                for g in range(per):
+                    rows = slice((part * per + g) * P, (part * per + g + 1) * P)
                     nc.tensor.matmul_mx(
                         out=acc[:, g, :],
                         lhsT=w2_codes[:, rows].bitcast(FP8X4),
@@ -168,28 +212,61 @@ def tile_picked_minmod_none_p_kernel(tc, x_words, x_scales, w1, gn, w2, offs, ea
                         start=True,
                         stop=True,
                     )
-                if c == len(CHUNKS) - 1 and half == 1:
+                if part == 1:
                     nc.vector.tensor_copy(res[:], acc[:])
                 else:
                     nc.scalar.copy(res[:], acc[:])
-                dst = out[half * per_bank * P : (half + 1) * per_bank * P, cols_of(c)].rearrange("(g p) n -> p g n", p=P)
+                dst = out[part * per * P : (part + 1) * per * P, r * P : (r + 1) * P].rearrange("(g p) n -> p g n", p=P)
                 nc.sync.dma_start(dst, res[:])
 
-        for i in range(len(units) + 2):
-            if i < len(units):
-                gather_east(*units[i])
-            if 1 <= i <= len(units):
-                clamp_low(*units[i - 1])
-            if i < len(units):
-                gather_west(*units[i])
-            if i >= 2:
-                add_centre(*units[i - 2])
-                if units[i - 2][1] == PACK - 1:
-                    interleave(units[i - 2][0])
-            if 1 <= i <= len(units):
-                clamp_high(*units[i - 1])
-            if i == 5:
-                nc.vector.quantize_mx(out=w2_codes[:].bitcast(FP8X4), scales=w2_scales[:], in_=w2_bf[:])
-            if i in (7, 10):
-                second_product((i - 7) // 3)
-        second_product(len(CHUNKS) - 1)
+        for t in range(3):
+            gather_east(0, t)
+            gather_west(0, t)
+        open_sum(0)
+        open_sum(1)
+        clamp_low(0, 0, 2)
+        gather_east(0, 3)
+        clamp_high(0, 0, 2)
+        gather_west(0, 3)
+        add_slope(0, 0, 2)
+        add_slope(1, 0, 2)
+        gather_east(1, 0, "low00")
+        clamp_low(0, 2, 4)
+        gather_east(1, 1)
+        clamp_high(0, 2, 4)
+        add_slope(0, 2, 4)
+        add_slope(1, 2, 4)
+        turn_back(0)
+        turn_back(1)
+        open_sum(2)
+        gather_west(1, 0, "a0")
+        gather_west(1, 1)
+        nc.vector.quantize_mx(out=w2_codes[:].bitcast(FP8X4), scales=w2_scales[:], in_=w2_bf[:])
+        for t in range(2, 4):
+            gather_east(1, t)
+            gather_west(1, t)
+        second_product(0)
+        gather_east(2, 0, "z_bf0")
+        clamp_low(1, 0, 4)
+        gather_east(2, 1)
+        clamp_high(1, 0, 4)
+        add_slope(2, 0, 4)
+        second_product(1)
+        turn_back(2)
+        gather_west(2, 0, "z_bf1")
+        gather_west(2, 1)
+        gather_east(2, 2)
+        gather_west(2, 2)
+        gather_east(2, 3)
+        clamp_low(2, 0, 3)
+        gather_west(2, 3)
+        clamp_high(2, 0, 3)
+        clamp_low(2, 3, 4)
+        add_centre(0)
+        add_centre(1)
+        clamp_high(2, 3, 4)
+        add_centre(2)
+        second_product(2)
+        add_centre(3)
+        interleave_last()
+        second_product(3)

@@ -20,7 +20,7 @@ P = 128
 PACK = 4
 HALF = S // 2
 CHUNKS = [(0, 256), (256, 128), (384, 128)]
-M_VECTOR = 64
+M_VECTOR = 60
 
 
 def tile_picked_minmod_none_p_kernel(tc, x_words, x_scales, w1, gn, w2, offs, east, west, out):
@@ -32,33 +32,32 @@ def tile_picked_minmod_none_p_kernel(tc, x_words, x_scales, w1, gn, w2, offs, ea
         offs_sb = sb.tile([P, S // 16], U16, name="offs_sb")
         east_sb = sb.tile([P, S // 16], U16, name="east_sb")
         west_sb = sb.tile([P, S // 16], U16, name="west_sb")
-        xw = sb.tile([P, T], U32, name="xw", align_bytes=64)
         xs = sb.tile([P, T], U8, name="xs", tag="xs", align_bytes=64)
         w1_raw = sb.tile([P, PACK, H], F32, name="w1_raw", tag="w_raw", align_bytes=64)
-        gn_sb = sb.tile([P, PACK], F32, name="gn_sb")
+        gn_sb = sb.tile([P, PACK], F32, name="gn_sb", tag="xw", align_bytes=64)
         g_pos = sb.tile([P, PACK], F32, name="g_pos")
         g_neg = sb.tile([P, PACK], F32, name="g_neg")
         ident = sb.tile([P, P], F32, name="ident", align_bytes=64)
 
         nc.vector.memset(xs[:].bitcast(I32), 0)
         nc.scalar.dma_start(gn_sb[:], gn.rearrange("(p t) o -> p (t o)", t=PACK))
-        nc.sync.dma_start(w1_raw[:], w1.rearrange("(p j) c -> p j c", j=PACK))
         nc.sync.dma_start(offs_sb[:], offs)
-        for q in range(4):
-            nc.scalar.dma_start(xs[32 * q : 32 * q + 4, :].bitcast(I32), x_scales[0, 4 * q : 4 * q + 4, :].bitcast(I32))
-        nc.sync.dma_start(xw[:].bitcast(I32), x_words[0].rearrange("p n t -> p (n t)").bitcast(I32))
+        nc.sync.dma_start(w1_raw[:], w1.rearrange("(p j) c -> p j c", j=PACK))
         nc.sync.dma_start(east_sb[:], east)
         nc.sync.dma_start(west_sb[:], west)
+        for q in range(4):
+            nc.sync.dma_start(xs[32 * q : 32 * q + 4, :].bitcast(I32), x_scales[0, 4 * q : 4 * q + 4, :].bitcast(I32))
+        nc.vector.tensor_scalar(g_pos[:], gn_sb[:], 0.5, None, ALU.mult)
+        nc.vector.tensor_scalar(g_neg[:], g_pos[:], -1.0, None, ALU.mult)
+        xw = sb.tile([P, T], U32, name="xw", tag="xw", align_bytes=64)
+        nc.sync.dma_start(xw[:].bitcast(I32), x_words[0].rearrange("p n t -> p (n t)").bitcast(I32))
         make_identity(nc, ident[:])
-
-        nc.scalar.activation(g_pos[:], gn_sb[:], COPY, scale=0.5)
-        nc.scalar.activation(g_neg[:], gn_sb[:], COPY, scale=-0.5)
 
         w1_bf = sb.tile([P, PACK * H], BF16, name="w1_bf", align_bytes=64)
         w1_dst = w1_bf[:].rearrange("p (t m j) -> p m t j", t=PACK, j=PACK)
         w1_src = w1_raw[:].rearrange("p j (m t) -> p m t j", t=PACK)
         nc.vector.tensor_copy(w1_dst[:, :M_VECTOR], w1_src[:, :M_VECTOR])
-        nc.scalar.copy(w1_dst[:, M_VECTOR:], w1_src[:, M_VECTOR:])
+        nc.scalar.activation(w1_dst[:, M_VECTOR:], w1_src[:, M_VECTOR:], COPY)
 
         w2_raw = sb.tile([P, PACK, N], F32, name="w2_raw", tag="w_raw", align_bytes=64)
         nc.sync.dma_start(w2_raw[:], w2.rearrange("(p j) c -> p j c", j=PACK))
@@ -66,24 +65,34 @@ def tile_picked_minmod_none_p_kernel(tc, x_words, x_scales, w1, gn, w2, offs, ea
         xg_scales = sb.tile([P, S], U8, name="xg_scales", align_bytes=64)
         nc.vector.tensor_copy(xg_scales[:], xs[:].indirect(offs_sb[:]))
 
-        w1_codes = sb.tile([P, H], U32, name="w1_codes", tag="w1_codes", align_bytes=64)
-        w1_scales = sb.tile([P, H], U8, name="w1_scales", align_bytes=64)
-        nc.vector.quantize_mx(out=w1_codes[:].bitcast(FP8X4), scales=w1_scales[:], in_=w1_bf[:])
+        w1_codes = {}
+        w1_scales = {}
 
-        xg = sb.tile([P, S], U32, name="xg", tag="xs", align_bytes=64)
+        def quantize_w1(t0, t1, codes_tag, scales_tag):
+            codes = sb.tile([P, (t1 - t0) * P], U32, name=f"w1_codes{t0}", tag=codes_tag, align_bytes=64)
+            scales = sb.tile([P, (t1 - t0) * P], U8, name=f"w1_scales{t0}", tag=scales_tag, align_bytes=64)
+            nc.vector.quantize_mx(out=codes[:].bitcast(FP8X4), scales=scales[:], in_=w1_bf[:, t0 * H : t1 * H])
+            for t in range(t0, t1):
+                w1_codes[t] = codes[:, (t - t0) * P : (t - t0 + 1) * P]
+                w1_scales[t] = scales[:, (t - t0) * P : (t - t0 + 1) * P]
+
+        quantize_w1(0, 2, "w1_codes0", "xs")
+
+        xg = sb.tile([P, S], U32, name="xg", align_bytes=64)
         for h in range(2):
             nc.vector.tensor_copy(xg[:, h * HALF : (h + 1) * HALF], xw[:].indirect(offs_sb[:, 16 * h : 16 * h + 16]))
+        quantize_w1(2, 4, "w1_codes2", "xw")
 
         u = [sb.tile([P, S], F32, name=f"u{t}", align_bytes=64) for t in range(PACK)]
         v = [sb.tile([P, S], F32, name=f"v{t}", align_bytes=64) for t in range(PACK)]
 
-        def first_product(acc, t, h):
+        def first_product(acc, t, cols):
             nc.tensor.matmul_mx(
                 out=acc,
-                lhsT=w1_codes[:, t * P : (t + 1) * P].bitcast(FP8X4),
-                lhsT_scale=w1_scales[:, t * P : (t + 1) * P],
-                rhs=xg[:, h * HALF : (h + 1) * HALF].bitcast(FP8X4),
-                rhs_scale=xg_scales[:, h * HALF : (h + 1) * HALF],
+                lhsT=w1_codes[t].bitcast(FP8X4),
+                lhsT_scale=w1_scales[t],
+                rhs=xg[:, cols].bitcast(FP8X4),
+                rhs_scale=xg_scales[:, cols],
                 start=True,
                 stop=True,
             )
@@ -94,8 +103,8 @@ def tile_picked_minmod_none_p_kernel(tc, x_words, x_scales, w1, gn, w2, offs, ea
 
         for h in range(2):
             acc = psum.tile([P, HALF], F32, name=f"y0{h}", tag=f"bank{h}")
-            first_product(acc[:], 0, h)
             cols = slice(h * HALF, (h + 1) * HALF)
+            first_product(acc[:], 0, cols)
             if h == 0:
                 nc.scalar.activation(u[0][:, cols], acc[:], COPY, scale=g_pos[:, 0:1])
             else:
@@ -103,11 +112,10 @@ def tile_picked_minmod_none_p_kernel(tc, x_words, x_scales, w1, gn, w2, offs, ea
             nc.scalar.activation(v[0][:, cols], acc[:], COPY, scale=g_neg[:, 0:1])
         for t in range(1, PACK):
             acc = psum.tile([P, S], F32, name=f"y{t}", tag=f"bank{t + 1}")
-            for h in range(2):
-                first_product(acc[:, h * HALF : (h + 1) * HALF], t, h)
+            first_product(acc[:], t, slice(0, S))
             leave(t, slice(0, S), acc[:])
 
-        w2_bf = sb.tile([P, PACK * N], BF16, name="w2_bf", tag="w1_codes", align_bytes=64)
+        w2_bf = sb.tile([P, PACK * N], BF16, name="w2_bf", tag="w1_codes2", align_bytes=64)
         w2_dst = w2_bf[:].rearrange("p (c i j) -> p c j i", i=4, j=PACK)
         w2_src = w2_raw[:].rearrange("p j (c i) -> p c j i", i=4)
         for part in range(2):
@@ -180,16 +188,28 @@ def tile_picked_minmod_none_p_kernel(tc, x_words, x_scales, w1, gn, w2, offs, ea
             src = pairs[:].rearrange("p e c -> p c e")
             nc.scalar.copy(dst, src)
 
-        z_last = sb.tile([P, PACK, P], BF16, name="z_last", align_bytes=64)
+        centre_planes = sb.tile([P, PACK, P], F32, name="centre_planes", align_bytes=64)
+        centre = sb.tile([P, P * PACK], F32, name="centre", align_bytes=64)
+        slope_last = sb.tile([P, PACK * P], F32, name="slope_last", align_bytes=64)
 
-        def add_centre(t):
-            nc.vector.scalar_tensor_tensor(z_last[:, t, :], u[t][:, 3 * P : 4 * P], 2.0, slope[3, t], ALU.mult, ALU.add)
+        def make_centre():
+            for t in range(PACK):
+                nc.scalar.activation(centre_planes[:, t, :], u[t][:, 3 * P : 4 * P], COPY, scale=2.0)
+            nc.scalar.copy(
+                centre[:].rearrange("p (c i t) -> p c t i", i=4, t=PACK),
+                centre_planes[:].rearrange("p t (c i) -> p c t i", i=4),
+            )
 
-        def interleave_last():
-            z_bf[3] = sb.tile([P, PACK * P], BF16, name="z_bf3", align_bytes=64)
-            nc.vector.tensor_copy(
-                z_bf[3][:].rearrange("p (c i t) -> p c t i", i=4, t=PACK),
-                z_last[:].rearrange("p t (c i) -> p c t i", i=4),
+        def clamp_high_last(t0, t1):
+            nc.vector.scalar_tensor_tensor(slope_last[:, t0 * P : t1 * P], b[2][:, planes(2, t0, t1)], 0.0, low[2, t0][:], ALU.max, ALU.min)
+
+        def add_centre_last(tag):
+            z_bf[3] = sb.tile([P, PACK * P], BF16, name="z_bf3", tag=tag, align_bytes=64)
+            nc.vector.tensor_tensor(
+                z_bf[3][:].rearrange("p (c t) -> p c t", t=PACK),
+                slope_last[:].rearrange("p (t c) -> p c t", t=PACK),
+                centre[:].rearrange("p (c t) -> p c t", t=PACK),
+                ALU.add,
             )
 
         def second_product(r):
@@ -222,6 +242,7 @@ def tile_picked_minmod_none_p_kernel(tc, x_words, x_scales, w1, gn, w2, offs, ea
         for t in range(3):
             gather_east(0, t)
             gather_west(0, t)
+        make_centre()
         open_sum(0)
         open_sum(1)
         clamp_low(0, 0, 2)
@@ -245,14 +266,14 @@ def tile_picked_minmod_none_p_kernel(tc, x_words, x_scales, w1, gn, w2, offs, ea
         for t in range(2, 4):
             gather_east(1, t)
             gather_west(1, t)
-        second_product(0)
-        gather_east(2, 0, "z_bf0")
+        gather_east(2, 0, "b0")
         clamp_low(1, 0, 4)
         gather_east(2, 1)
-        clamp_high(1, 0, 4)
+        second_product(0)
+        clamp_high(1, 0, 4, "z_bf0")
         add_slope(2, 0, 4)
-        second_product(1)
         turn_back(2)
+        second_product(1)
         gather_west(2, 0, "z_bf1")
         gather_west(2, 1)
         gather_east(2, 2)
@@ -260,13 +281,9 @@ def tile_picked_minmod_none_p_kernel(tc, x_words, x_scales, w1, gn, w2, offs, ea
         gather_east(2, 3)
         clamp_low(2, 0, 3)
         gather_west(2, 3)
-        clamp_high(2, 0, 3)
+        clamp_high_last(0, 3)
         clamp_low(2, 3, 4)
-        add_centre(0)
-        add_centre(1)
-        clamp_high(2, 3, 4)
-        add_centre(2)
         second_product(2)
-        add_centre(3)
-        interleave_last()
+        clamp_high_last(3, 4)
+        add_centre_last("z_bf2")
         second_product(3)

@@ -1,7 +1,6 @@
 from contextlib import ExitStack
 
 import concourse.mybir as mybir
-from concourse.masks import make_identity
 
 K, T, S, N, H = 512, 2048, 512, 512, 512
 FLOPS = 2 * K * H * S + 2 * H * N * S
@@ -19,7 +18,6 @@ COPY = mybir.ActivationFunctionType.Copy
 P = 128
 PACK = 4
 HALF = S // 2
-CHUNKS = [(0, 256), (256, 128), (384, 128)]
 M_VECTOR = 60
 
 
@@ -35,9 +33,9 @@ def tile_picked_minmod_none_p_kernel(tc, x_words, x_scales, w1, gn, w2, offs, ea
         xs = sb.tile([P, T], U8, name="xs", tag="xs", align_bytes=64)
         w1_raw = sb.tile([P, PACK, H], F32, name="w1_raw", tag="w_raw", align_bytes=64)
         gn_sb = sb.tile([P, PACK], F32, name="gn_sb", tag="xw", align_bytes=64)
-        g_pos = sb.tile([P, PACK], F32, name="g_pos")
-        g_neg = sb.tile([P, PACK], F32, name="g_neg")
-        ident = sb.tile([P, P], F32, name="ident", align_bytes=64)
+        gain = sb.tile([P, PACK], F32, name="gain")
+        g_pos = sb.tile([P, 1], F32, name="g_pos")
+        g_neg = sb.tile([P, 1], F32, name="g_neg")
 
         nc.vector.memset(xs[:].bitcast(I32), 0)
         nc.scalar.dma_start(gn_sb[:], gn.rearrange("(p t) o -> p (t o)", t=PACK))
@@ -47,11 +45,11 @@ def tile_picked_minmod_none_p_kernel(tc, x_words, x_scales, w1, gn, w2, offs, ea
         nc.sync.dma_start(west_sb[:], west)
         for q in range(4):
             nc.sync.dma_start(xs[32 * q : 32 * q + 4, :].bitcast(I32), x_scales[0, 4 * q : 4 * q + 4, :].bitcast(I32))
-        nc.vector.tensor_scalar(g_pos[:], gn_sb[:], 0.5, None, ALU.mult)
-        nc.vector.tensor_scalar(g_neg[:], g_pos[:], -1.0, None, ALU.mult)
+        nc.vector.tensor_copy(gain[:], gn_sb[:])
+        nc.vector.tensor_scalar(g_pos[:], gn_sb[:, 0:1], 0.5, None, ALU.mult)
+        nc.vector.tensor_scalar(g_neg[:], gn_sb[:, 0:1], -0.5, None, ALU.mult)
         xw = sb.tile([P, T], U32, name="xw", tag="xw", align_bytes=64)
         nc.sync.dma_start(xw[:].bitcast(I32), x_words[0].rearrange("p n t -> p (n t)").bitcast(I32))
-        make_identity(nc, ident[:])
 
         w1_bf = sb.tile([P, PACK * H], BF16, name="w1_bf", align_bytes=64)
         w1_dst = w1_bf[:].rearrange("p (t m j) -> p m t j", t=PACK, j=PACK)
@@ -59,8 +57,9 @@ def tile_picked_minmod_none_p_kernel(tc, x_words, x_scales, w1, gn, w2, offs, ea
         nc.vector.tensor_copy(w1_dst[:, :M_VECTOR], w1_src[:, :M_VECTOR])
         nc.scalar.activation(w1_dst[:, M_VECTOR:], w1_src[:, M_VECTOR:], COPY)
 
-        w2_raw = sb.tile([P, PACK, N], F32, name="w2_raw", tag="w_raw", align_bytes=64)
-        nc.sync.dma_start(w2_raw[:], w2.rearrange("(p j) c -> p j c", j=PACK))
+        w2_raw = sb.tile([P, 2, PACK, N // 2], F32, name="w2_raw", tag="w_raw", align_bytes=64)
+        for h in range(2):
+            nc.sync.dma_start(w2_raw[:, h], w2[:, h * HALF : (h + 1) * HALF].rearrange("(p j) c -> p j c", j=PACK))
 
         xg_scales = sb.tile([P, S], U8, name="xg_scales", align_bytes=64)
         nc.vector.tensor_copy(xg_scales[:], xs[:].indirect(offs_sb[:]))
@@ -84,7 +83,8 @@ def tile_picked_minmod_none_p_kernel(tc, x_words, x_scales, w1, gn, w2, offs, ea
         quantize_w1(2, 4, "w1_codes2", "xw")
 
         u = [sb.tile([P, S], F32, name=f"u{t}", align_bytes=64) for t in range(PACK)]
-        v = [sb.tile([P, S], F32, name=f"v{t}", align_bytes=64) for t in range(PACK)]
+        v0 = sb.tile([P, S], F32, name="v0", align_bytes=64)
+        centre = sb.tile([P, PACK, S], F32, name="centre", align_bytes=64)
 
         def first_product(acc, t, cols):
             nc.tensor.matmul_mx(
@@ -97,193 +97,154 @@ def tile_picked_minmod_none_p_kernel(tc, x_words, x_scales, w1, gn, w2, offs, ea
                 stop=True,
             )
 
-        def leave(t, cols, acc):
-            nc.scalar.activation(u[t][:, cols], acc, COPY, scale=g_pos[:, t : t + 1])
-            nc.scalar.activation(v[t][:, cols], acc, COPY, scale=g_neg[:, t : t + 1])
-
         for h in range(2):
             acc = psum.tile([P, HALF], F32, name=f"y0{h}", tag=f"bank{h}")
             cols = slice(h * HALF, (h + 1) * HALF)
             first_product(acc[:], 0, cols)
+            nc.scalar.activation(u[0][:, cols], acc[:], COPY, scale=g_pos[:])
             if h == 0:
-                nc.scalar.activation(u[0][:, cols], acc[:], COPY, scale=g_pos[:, 0:1])
+                nc.vector.tensor_scalar(v0[:, cols], acc[:], g_neg[:], None, ALU.mult)
             else:
-                nc.vector.tensor_scalar(u[0][:, cols], acc[:], g_pos[:, 0:1], None, ALU.mult)
-            nc.scalar.activation(v[0][:, cols], acc[:], COPY, scale=g_neg[:, 0:1])
-        for t in range(1, PACK):
-            acc = psum.tile([P, S], F32, name=f"y{t}", tag=f"bank{t + 1}")
-            first_product(acc[:], t, slice(0, S))
-            leave(t, slice(0, S), acc[:])
+                nc.scalar.activation(v0[:, cols], acc[:], COPY, scale=g_neg[:])
 
-        w2_bf = sb.tile([P, PACK * N], BF16, name="w2_bf", tag="w1_codes2", align_bytes=64)
-        w2_dst = w2_bf[:].rearrange("p (c i j) -> p c j i", i=4, j=PACK)
-        w2_src = w2_raw[:].rearrange("p j (c i) -> p c j i", i=4)
-        for part in range(2):
-            nc.scalar.copy(w2_dst[:, 64 * part : 64 * part + 64], w2_src[:, 64 * part : 64 * part + 64])
+        w2_bf = [sb.tile([P, PACK * HALF], BF16, name=f"w2_bf{h}", align_bytes=64) for h in range(2)]
         w2_codes = sb.tile([P, N], U32, name="w2_codes", align_bytes=64)
         w2_scales = sb.tile([P, N], U8, name="w2_scales", align_bytes=64)
 
-        a = {}
-        b = {}
-        low = {}
-        slope = {}
+        def round_w2(h, copy):
+            copy(
+                w2_bf[h][:].rearrange("p (c i j) -> p c j i", i=4, j=PACK),
+                w2_raw[:, h].rearrange("p j (c i) -> p c j i", i=4),
+            )
 
-        def planes(c, t0, t1):
-            return slice(t0 * CHUNKS[c][1], t1 * CHUNKS[c][1])
+        def quantize_w2(h):
+            cols = slice(h * HALF, (h + 1) * HALF)
+            nc.vector.quantize_mx(out=w2_codes[:, cols].bitcast(FP8X4), scales=w2_scales[:, cols], in_=w2_bf[h][:])
 
-        def cells(c):
-            return slice(CHUNKS[c][0], CHUNKS[c][0] + CHUNKS[c][1])
+        round_w2(0, nc.vector.tensor_copy)
 
-        def list_cols(c):
-            return slice(CHUNKS[c][0] // 16, (CHUNKS[c][0] + CHUNKS[c][1]) // 16)
+        def leave(t):
+            acc = psum.tile([P, S], F32, name=f"y{t}", tag=f"bank{t + 1}")
+            first_product(acc[:], t, slice(0, S))
+            nc.scalar.activation(u[t][:], acc[:], COPY, scale=gain[:, t : t + 1])
+            nc.sync.dma_start(centre[:, t, :], u[t][:])
 
-        def gather_east(c, t, tag=None):
-            if t == 0:
-                b[c] = sb.tile([P, PACK * CHUNKS[c][1]], F32, name=f"b{c}", tag=tag or f"b{c}", align_bytes=64)
-            nc.vector.tensor_tensor(b[c][:, planes(c, t, t + 1)], u[t][:].indirect(east_sb[:, list_cols(c)]), v[t][:, cells(c)], ALU.add)
+        a = sb.tile([P, PACK, S], F32, name="a", align_bytes=64)
+        b = sb.tile([P, PACK, S], F32, name="b", align_bytes=64)
+        from_west = sb.tile([P, PACK - 1, S], F32, name="from_west", align_bytes=64)
+        from_east = sb.tile([P, PACK - 1, S], F32, name="from_east", align_bytes=64)
+        low = sb.tile([P, PACK, S], F32, name="low", align_bytes=64)
+        slope = sb.tile([P, PACK, S], F32, name="slope", align_bytes=64)
 
-        def gather_west(c, t, tag=None):
-            if t == 0:
-                a[c] = sb.tile([P, PACK * CHUNKS[c][1]], F32, name=f"a{c}", tag=tag or f"a{c}", align_bytes=64)
-            nc.vector.tensor_tensor(a[c][:, planes(c, t, t + 1)], v[t][:].indirect(west_sb[:, list_cols(c)]), u[t][:, cells(c)], ALU.add)
+        def entries(cells):
+            return slice(cells.start // 16, cells.stop // 16)
 
-        def clamp_low(c, t0, t1, tag=None):
-            name = f"low{c}{t0}"
-            low[c, t0] = sb.tile([P, (t1 - t0) * CHUNKS[c][1]], F32, name=name, tag=tag or name, align_bytes=64)
-            nc.vector.scalar_tensor_tensor(low[c, t0][:], b[c][:, planes(c, t0, t1)], 0.0, a[c][:, planes(c, t0, t1)], ALU.min, ALU.max)
+        def fused_gathers(cells):
+            nc.vector.tensor_tensor(b[:, 0, cells], u[0][:].indirect(east_sb[:, entries(cells)]), v0[:, cells], ALU.add)
+            nc.vector.tensor_tensor(a[:, 0, cells], v0[:].indirect(west_sb[:, entries(cells)]), u[0][:, cells], ALU.add)
 
-        def clamp_high(c, t0, t1, tag=None):
-            name = f"slope{c}{t0}"
-            width = CHUNKS[c][1]
-            tile = sb.tile([P, (t1 - t0) * width], F32, name=name, tag=tag or name, align_bytes=64)
-            nc.vector.scalar_tensor_tensor(tile[:], b[c][:, planes(c, t0, t1)], 0.0, low[c, t0][:], ALU.max, ALU.min)
-            for t in range(t0, t1):
-                for i in range(width // P):
-                    slope[CHUNKS[c][0] // P + i, t] = tile[:, (t - t0) * width + i * P : (t - t0) * width + (i + 1) * P]
+        def plain_gathers(t, cells):
+            nc.scalar.activation(from_west[:, t - 1, cells], u[t][:].indirect(west_sb[:, entries(cells)]), COPY, scale=-0.5)
+            nc.scalar.activation(from_east[:, t - 1, cells], u[t][:].indirect(east_sb[:, entries(cells)]), COPY, scale=0.5)
 
-        zt = {}
+        def differences(t, cells):
+            nc.vector.scalar_tensor_tensor(a[:, t, cells], u[t][:, cells], 0.5, from_west[:, t - 1, cells], ALU.mult, ALU.add)
+            nc.vector.scalar_tensor_tensor(b[:, t, cells], u[t][:, cells], -0.5, from_east[:, t - 1, cells], ALU.mult, ALU.add)
+
+        def west_difference(cells):
+            nc.vector.scalar_tensor_tensor(a[:, 1:, cells], centre[:, 1:, cells], 0.5, from_west[:, :, cells], ALU.mult, ALU.add)
+
+        def east_difference(cells):
+            nc.vector.scalar_tensor_tensor(b[:, 1:, cells], centre[:, 1:, cells], -0.5, from_east[:, :, cells], ALU.mult, ALU.add)
+
+        def clamp_low(t0, t1, cells):
+            nc.vector.scalar_tensor_tensor(low[:, t0:t1, cells], b[:, t0:t1, cells], 0.0, a[:, t0:t1, cells], ALU.min, ALU.max)
+
+        def clamp_high(t0, t1, cells):
+            nc.vector.scalar_tensor_tensor(slope[:, t0:t1, cells], b[:, t0:t1, cells], 0.0, low[:, t0:t1, cells], ALU.max, ALU.min)
+
         z_bf = {}
+        z_codes = {}
+        z_scales = {}
 
-        def open_sum(r):
-            zt[r] = psum.tile([P, PACK, P], F32, name=f"zt{r}", tag=f"bank{(5, 6, 0, 1)[r]}")
-            for t in range(PACK):
-                for rep in range(2):
-                    nc.tensor.matmul(zt[r][:, t, :], u[t][:, r * P : (r + 1) * P], ident[:], start=(t == 0 and rep == 0), stop=False, is_transpose=True)
-
-        def add_slope(r, t0, t1):
-            for t in range(t0, t1):
-                nc.tensor.matmul(zt[r][:, t, :], slope[r, t], ident[:], start=False, stop=(t == PACK - 1), is_transpose=True)
-
-        def turn_back(r):
-            rounded = sb.tile([P, PACK * P], BF16, name=f"rounded{r}", align_bytes=64)
-            nc.scalar.copy(
-                rounded[:].rearrange("c (e p k) -> c e p k", e=2, k=2),
-                zt[r][:].rearrange("c (e k) p -> c e p k", k=2),
-            )
-            pairs = psum.tile([P, 2, P], F32, name=f"pairs{r}", tag=f"bank{(7, 2)[r % 2]}")
-            for e in range(2):
-                nc.tensor.transpose(pairs[:, e, :], rounded[:].bitcast(F32)[:, e * P : (e + 1) * P], ident[:])
-            z_bf[r] = sb.tile([P, PACK * P], BF16, name=f"z_bf{r}", tag=f"z_bf{r}", align_bytes=64)
-            dst = z_bf[r][:].bitcast(F32).rearrange("p (c e) -> p c e", e=2)
-            src = pairs[:].rearrange("p e c -> p c e")
-            nc.scalar.copy(dst, src)
-
-        centre_planes = sb.tile([P, PACK, P], F32, name="centre_planes", align_bytes=64)
-        centre = sb.tile([P, P * PACK], F32, name="centre", align_bytes=64)
-        slope_last = sb.tile([P, PACK * P], F32, name="slope_last", align_bytes=64)
-
-        def make_centre():
-            for t in range(PACK):
-                nc.scalar.activation(centre_planes[:, t, :], u[t][:, 3 * P : 4 * P], COPY, scale=2.0)
-            nc.scalar.copy(
-                centre[:].rearrange("p (c i t) -> p c t i", i=4, t=PACK),
-                centre_planes[:].rearrange("p t (c i) -> p c t i", i=4),
-            )
-
-        def clamp_high_last(t0, t1):
-            nc.vector.scalar_tensor_tensor(slope_last[:, t0 * P : t1 * P], b[2][:, planes(2, t0, t1)], 0.0, low[2, t0][:], ALU.max, ALU.min)
-
-        def add_centre_last(tag):
-            z_bf[3] = sb.tile([P, PACK * P], BF16, name="z_bf3", tag=tag, align_bytes=64)
+        def add_centre(cells):
+            width = cells.stop - cells.start
+            z_bf[cells.start] = sb.tile([P, PACK * width], BF16, name=f"z_bf{cells.start}", align_bytes=64)
             nc.vector.tensor_tensor(
-                z_bf[3][:].rearrange("p (c t) -> p c t", t=PACK),
-                slope_last[:].rearrange("p (t c) -> p c t", t=PACK),
-                centre[:].rearrange("p (c t) -> p c t", t=PACK),
+                z_bf[cells.start][:].rearrange("p (c i t) -> p c t i", i=2, t=PACK),
+                slope[:, :, cells].rearrange("p t (c i) -> p c t i", i=2),
+                centre[:, :, cells].rearrange("p t (c i) -> p c t i", i=2),
                 ALU.add,
             )
 
-        def second_product(r):
-            codes = sb.tile([P, P], U32, name=f"z_codes{r}", align_bytes=64)
-            scales = sb.tile([P, P], U8, name=f"z_scales{r}", align_bytes=64)
-            nc.vector.quantize_mx(out=codes[:].bitcast(FP8X4), scales=scales[:], in_=z_bf[r][:])
-            parts = 2 if r == 3 else 1
-            per = PACK // parts
-            for part in range(parts):
-                acc = psum.tile([P, per, P], F32, name=f"o{r}{part}", tag=f"bank{(3, 4, 5, 6, 1)[r + part]}")
-                res = sb.tile([P, per, P], F32, name=f"res{r}{part}", align_bytes=64)
-                for g in range(per):
-                    rows = slice((part * per + g) * P, (part * per + g + 1) * P)
-                    nc.tensor.matmul_mx(
-                        out=acc[:, g, :],
-                        lhsT=w2_codes[:, rows].bitcast(FP8X4),
-                        lhsT_scale=w2_scales[:, rows],
-                        rhs=codes[:].bitcast(FP8X4),
-                        rhs_scale=scales[:],
-                        start=True,
-                        stop=True,
-                    )
-                if part == 1:
-                    nc.vector.tensor_copy(res[:], acc[:])
-                else:
-                    nc.scalar.copy(res[:], acc[:])
-                dst = out[part * per * P : (part + 1) * per * P, r * P : (r + 1) * P].rearrange("(g p) n -> p g n", p=P)
-                nc.sync.dma_start(dst, res[:])
+        def quantize_z(cells):
+            width = cells.stop - cells.start
+            z_codes[cells.start] = sb.tile([P, width], U32, name=f"z_codes{cells.start}", align_bytes=64)
+            z_scales[cells.start] = sb.tile([P, width], U8, name=f"z_scales{cells.start}", align_bytes=64)
+            nc.vector.quantize_mx(out=z_codes[cells.start][:].bitcast(FP8X4), scales=z_scales[cells.start][:], in_=z_bf[cells.start][:])
 
-        for t in range(3):
-            gather_east(0, t)
-            gather_west(0, t)
-        make_centre()
-        open_sum(0)
-        open_sum(1)
-        clamp_low(0, 0, 2)
-        gather_east(0, 3)
-        clamp_high(0, 0, 2)
-        gather_west(0, 3)
-        add_slope(0, 0, 2)
-        add_slope(1, 0, 2)
-        gather_east(1, 0, "low00")
-        clamp_low(0, 2, 4)
-        gather_east(1, 1)
-        clamp_high(0, 2, 4)
-        add_slope(0, 2, 4)
-        add_slope(1, 2, 4)
-        turn_back(0)
-        turn_back(1)
-        open_sum(2)
-        gather_west(1, 0, "a0")
-        gather_west(1, 1)
-        nc.vector.quantize_mx(out=w2_codes[:].bitcast(FP8X4), scales=w2_scales[:], in_=w2_bf[:])
-        for t in range(2, 4):
-            gather_east(1, t)
-            gather_west(1, t)
-        gather_east(2, 0, "b0")
-        clamp_low(1, 0, 4)
-        gather_east(2, 1)
-        second_product(0)
-        clamp_high(1, 0, 4, "z_bf0")
-        add_slope(2, 0, 4)
-        turn_back(2)
-        second_product(1)
-        gather_west(2, 0, "z_bf1")
-        gather_west(2, 1)
-        gather_east(2, 2)
-        gather_west(2, 2)
-        gather_east(2, 3)
-        clamp_low(2, 0, 3)
-        gather_west(2, 3)
-        clamp_high_last(0, 3)
-        clamp_low(2, 3, 4)
-        second_product(2)
-        clamp_high_last(3, 4)
-        add_centre_last("z_bf2")
-        second_product(3)
+        def second_product(cells, g0, g1, bank, copy):
+            width = cells.stop - cells.start
+            acc = psum.tile([P, g1 - g0, width], F32, name=f"o{cells.start}_{g0}", tag=f"bank{bank}")
+            res = sb.tile([P, g1 - g0, width], F32, name=f"res{cells.start}_{g0}", align_bytes=64)
+            for g in range(g0, g1):
+                rows = slice(g * P, (g + 1) * P)
+                nc.tensor.matmul_mx(
+                    out=acc[:, g - g0, :],
+                    lhsT=w2_codes[:, rows].bitcast(FP8X4),
+                    lhsT_scale=w2_scales[:, rows],
+                    rhs=z_codes[cells.start][:].bitcast(FP8X4),
+                    rhs_scale=z_scales[cells.start][:],
+                    start=True,
+                    stop=True,
+                )
+            copy(res[:], acc[:])
+            nc.sync.dma_start(out[g0 * P : g1 * P, cells].rearrange("(g p) n -> p g n", p=P), res[:])
+
+        first = slice(0, 256)
+        second = slice(256, 512)
+        third_block = slice(256, 384)
+        last_block = slice(384, 512)
+
+        leave(1)
+        leave(2)
+        fused_gathers(first)
+        plain_gathers(1, first)
+        leave(3)
+        fused_gathers(second)
+        plain_gathers(2, first)
+        plain_gathers(3, first)
+        nc.vector.tensor_scalar(centre[:, 0, :], u[0][:], 2.0, None, ALU.mult)
+        differences(1, first)
+        quantize_w2(0)
+        clamp_low(0, 2, first)
+        differences(2, first)
+        round_w2(1, nc.scalar.copy)
+        for t in range(1, PACK):
+            plain_gathers(t, third_block)
+        for t in range(1, PACK):
+            plain_gathers(t, last_block)
+        clamp_high(0, 2, first)
+        differences(3, first)
+        quantize_w2(1)
+        clamp_low(2, 4, first)
+        west_difference(third_block)
+        clamp_high(2, 4, first)
+        east_difference(third_block)
+        add_centre(first)
+        clamp_low(0, 4, third_block)
+        quantize_z(first)
+        second_product(first, 0, 2, 5, nc.scalar.copy)
+        second_product(first, 2, 4, 6, nc.scalar.copy)
+        clamp_high(0, 4, third_block)
+        west_difference(last_block)
+        add_centre(third_block)
+        east_difference(last_block)
+        quantize_z(third_block)
+        second_product(third_block, 0, 4, 7, nc.scalar.copy)
+        clamp_low(0, 4, last_block)
+        clamp_high(0, 4, last_block)
+        add_centre(last_block)
+        quantize_z(last_block)
+        second_product(last_block, 0, 2, 0, nc.scalar.copy)
+        second_product(last_block, 2, 4, 1, nc.vector.tensor_copy)

@@ -1,6 +1,7 @@
 from contextlib import ExitStack
 
 import concourse.mybir as mybir
+from concourse.masks import make_identity
 
 K, T, S, N, H = 512, 2048, 512, 512, 512
 FLOPS = 2 * K * H * S + 2 * H * N * S
@@ -19,12 +20,14 @@ P = 128
 PACK = 4
 HALF = S // 2
 M_VECTOR = 60
+W2_SCALAR = 36
 
 
 def tile_picked_minmod_none_p_kernel(tc, x_words, x_scales, w1, gn, w2, offs, east, west, out):
     nc = tc.nc
     with ExitStack() as ctx:
         sb = ctx.enter_context(tc.tile_pool(name="sb", bufs=1))
+        late = ctx.enter_context(tc.tile_pool(name="late", bufs=1))
         psum = ctx.enter_context(tc.psum_pool(name="psum", bufs=1))
 
         offs_sb = sb.tile([P, S // 16], U16, name="offs_sb")
@@ -32,24 +35,26 @@ def tile_picked_minmod_none_p_kernel(tc, x_words, x_scales, w1, gn, w2, offs, ea
         west_sb = sb.tile([P, S // 16], U16, name="west_sb")
         xs = sb.tile([P, T], U8, name="xs", tag="xs", align_bytes=64)
         w1_raw = sb.tile([P, PACK, H], F32, name="w1_raw", tag="w_raw", align_bytes=64)
-        gn_sb = sb.tile([P, PACK], F32, name="gn_sb", tag="xw", align_bytes=64)
+        gn_sb = late.tile([P, 32], F32, name="gn_sb", offset=4 * T - 64, align_bytes=64)
         gain = sb.tile([P, PACK], F32, name="gain")
         g_pos = sb.tile([P, 1], F32, name="g_pos")
         g_neg = sb.tile([P, 1], F32, name="g_neg")
+        ident = sb.tile([P, P], F32, name="ident", align_bytes=64)
 
         nc.vector.memset(xs[:].bitcast(I32), 0)
-        nc.scalar.dma_start(gn_sb[:], gn.rearrange("(p t) o -> p (t o)", t=PACK))
+        nc.scalar.dma_start(gn_sb[:, :PACK], gn.rearrange("(p t) o -> p (t o)", t=PACK))
         nc.sync.dma_start(offs_sb[:], offs)
         nc.sync.dma_start(w1_raw[:], w1.rearrange("(p j) c -> p j c", j=PACK))
         nc.sync.dma_start(east_sb[:], east)
         nc.sync.dma_start(west_sb[:], west)
         for q in range(4):
             nc.sync.dma_start(xs[32 * q : 32 * q + 4, :].bitcast(I32), x_scales[0, 4 * q : 4 * q + 4, :].bitcast(I32))
-        nc.vector.tensor_copy(gain[:], gn_sb[:])
-        nc.vector.tensor_scalar(g_pos[:], gn_sb[:, 0:1], 0.5, None, ALU.mult)
-        nc.vector.tensor_scalar(g_neg[:], gn_sb[:, 0:1], -0.5, None, ALU.mult)
-        xw = sb.tile([P, T], U32, name="xw", tag="xw", align_bytes=64)
+        nc.vector.tensor_copy(gain[:], gn_sb[:, :PACK])
+        nc.vector.tensor_scalar(g_pos[:], gain[:, 0:1], 0.5, None, ALU.mult)
+        nc.vector.tensor_scalar(g_neg[:], gain[:, 0:1], -0.5, None, ALU.mult)
+        xw = late.tile([P, T], U32, name="xw", offset=0, align_bytes=64)
         nc.sync.dma_start(xw[:].bitcast(I32), x_words[0].rearrange("p n t -> p (n t)").bitcast(I32))
+        make_identity(nc, ident[:])
 
         w1_bf = sb.tile([P, PACK * H], BF16, name="w1_bf", align_bytes=64)
         w1_dst = w1_bf[:].rearrange("p (t m j) -> p m t j", t=PACK, j=PACK)
@@ -57,7 +62,7 @@ def tile_picked_minmod_none_p_kernel(tc, x_words, x_scales, w1, gn, w2, offs, ea
         nc.vector.tensor_copy(w1_dst[:, :M_VECTOR], w1_src[:, :M_VECTOR])
         nc.scalar.activation(w1_dst[:, M_VECTOR:], w1_src[:, M_VECTOR:], COPY)
 
-        w2_raw = sb.tile([P, 2, PACK, N // 2], F32, name="w2_raw", tag="w_raw", align_bytes=64)
+        w2_raw = late.tile([P, 2, PACK, N // 2], F32, name="w2_raw", offset=4 * T, align_bytes=64)
         for h in range(2):
             nc.sync.dma_start(w2_raw[:, h], w2[:, h * HALF : (h + 1) * HALF].rearrange("(p j) c -> p j c", j=PACK))
 
@@ -67,24 +72,22 @@ def tile_picked_minmod_none_p_kernel(tc, x_words, x_scales, w1, gn, w2, offs, ea
         w1_codes = {}
         w1_scales = {}
 
-        def quantize_w1(t0, t1, codes_tag, scales_tag):
-            codes = sb.tile([P, (t1 - t0) * P], U32, name=f"w1_codes{t0}", tag=codes_tag, align_bytes=64)
-            scales = sb.tile([P, (t1 - t0) * P], U8, name=f"w1_scales{t0}", tag=scales_tag, align_bytes=64)
+        def quantize_w1(t0, t1, scales):
+            codes = sb.tile([P, (t1 - t0) * P], U32, name=f"w1_codes{t0}", align_bytes=64)
             nc.vector.quantize_mx(out=codes[:].bitcast(FP8X4), scales=scales[:], in_=w1_bf[:, t0 * H : t1 * H])
             for t in range(t0, t1):
                 w1_codes[t] = codes[:, (t - t0) * P : (t - t0 + 1) * P]
                 w1_scales[t] = scales[:, (t - t0) * P : (t - t0 + 1) * P]
 
-        quantize_w1(0, 2, "w1_codes0", "xs")
+        quantize_w1(0, 2, sb.tile([P, 2 * P], U8, name="w1_scales0", tag="xs", align_bytes=64))
 
         xg = sb.tile([P, S], U32, name="xg", align_bytes=64)
         for h in range(2):
             nc.vector.tensor_copy(xg[:, h * HALF : (h + 1) * HALF], xw[:].indirect(offs_sb[:, 16 * h : 16 * h + 16]))
-        quantize_w1(2, 4, "w1_codes2", "xw")
+        quantize_w1(2, 4, late.tile([P, 2 * P], U8, name="w1_scales2", offset=0, align_bytes=64))
 
         u = [sb.tile([P, S], F32, name=f"u{t}", align_bytes=64) for t in range(PACK)]
         v0 = sb.tile([P, S], F32, name="v0", align_bytes=64)
-        centre = sb.tile([P, PACK, S], F32, name="centre", align_bytes=64)
 
         def first_product(acc, t, cols):
             nc.tensor.matmul_mx(
@@ -97,6 +100,23 @@ def tile_picked_minmod_none_p_kernel(tc, x_words, x_scales, w1, gn, w2, offs, ea
                 stop=True,
             )
 
+        w2_bf = [sb.tile([P, PACK * HALF], BF16, name=f"w2_bf{h}", align_bytes=64) for h in range(2)]
+        w2_codes = sb.tile([P, N], U32, name="w2_codes", align_bytes=64)
+        w2_scales = {}
+
+        def round_w2(h, c0, c1, copy):
+            copy(
+                w2_bf[h][:].rearrange("p (c i j) -> p c j i", i=4, j=PACK)[:, c0:c1],
+                w2_raw[:, h].rearrange("p j (c i) -> p c j i", i=4)[:, c0:c1],
+            )
+
+        def quantize_w2(h, tag):
+            w2_scales[h] = sb.tile([P, HALF], U8, name=f"w2_scales{h}", tag=tag, align_bytes=64)
+            nc.vector.quantize_mx(out=w2_codes[:, h * HALF : (h + 1) * HALF].bitcast(FP8X4), scales=w2_scales[h][:], in_=w2_bf[h][:])
+
+        round_w2(0, 0, W2_SCALAR, nc.scalar.copy)
+        round_w2(0, W2_SCALAR, 64, nc.vector.tensor_copy)
+
         for h in range(2):
             acc = psum.tile([P, HALF], F32, name=f"y0{h}", tag=f"bank{h}")
             cols = slice(h * HALF, (h + 1) * HALF)
@@ -104,64 +124,69 @@ def tile_picked_minmod_none_p_kernel(tc, x_words, x_scales, w1, gn, w2, offs, ea
             nc.scalar.activation(u[0][:, cols], acc[:], COPY, scale=g_pos[:])
             if h == 0:
                 nc.vector.tensor_scalar(v0[:, cols], acc[:], g_neg[:], None, ALU.mult)
-            else:
-                nc.scalar.activation(v0[:, cols], acc[:], COPY, scale=g_neg[:])
 
-        w2_bf = [sb.tile([P, PACK * HALF], BF16, name=f"w2_bf{h}", align_bytes=64) for h in range(2)]
-        w2_codes = sb.tile([P, N], U32, name="w2_codes", align_bytes=64)
-        w2_scales = sb.tile([P, N], U8, name="w2_scales", align_bytes=64)
-
-        def round_w2(h, copy):
-            copy(
-                w2_bf[h][:].rearrange("p (c i j) -> p c j i", i=4, j=PACK),
-                w2_raw[:, h].rearrange("p j (c i) -> p c j i", i=4),
-            )
-
-        def quantize_w2(h):
-            cols = slice(h * HALF, (h + 1) * HALF)
-            nc.vector.quantize_mx(out=w2_codes[:, cols].bitcast(FP8X4), scales=w2_scales[:, cols], in_=w2_bf[h][:])
-
-        round_w2(0, nc.vector.tensor_copy)
+        round_w2(1, 0, 64, nc.vector.tensor_copy)
 
         def leave(t):
             acc = psum.tile([P, S], F32, name=f"y{t}", tag=f"bank{t + 1}")
             first_product(acc[:], t, slice(0, S))
             nc.scalar.activation(u[t][:], acc[:], COPY, scale=gain[:, t : t + 1])
-            nc.sync.dma_start(centre[:, t, :], u[t][:])
 
-        a = sb.tile([P, PACK, S], F32, name="a", align_bytes=64)
-        b = sb.tile([P, PACK, S], F32, name="b", align_bytes=64)
-        from_west = sb.tile([P, PACK - 1, S], F32, name="from_west", align_bytes=64)
-        from_east = sb.tile([P, PACK - 1, S], F32, name="from_east", align_bytes=64)
+        a = {0: sb.tile([P, PACK, HALF], F32, name="a0", align_bytes=64)}
+        b = {h: sb.tile([P, PACK, HALF], F32, name=f"b{h}", align_bytes=64) for h in range(2)}
         low = sb.tile([P, PACK, S], F32, name="low", align_bytes=64)
         slope = sb.tile([P, PACK, S], F32, name="slope", align_bytes=64)
+        early_west = {}
+        early_east = {}
+        late_west = sb.tile([P, PACK - 1, HALF], F32, name="late_west", align_bytes=64)
+        late_east = sb.tile([P, PACK - 1, HALF], F32, name="late_east", align_bytes=64)
 
         def entries(cells):
             return slice(cells.start // 16, cells.stop // 16)
 
-        def fused_gathers(cells):
-            nc.vector.tensor_tensor(b[:, 0, cells], u[0][:].indirect(east_sb[:, entries(cells)]), v0[:, cells], ALU.add)
-            nc.vector.tensor_tensor(a[:, 0, cells], v0[:].indirect(west_sb[:, entries(cells)]), u[0][:, cells], ALU.add)
+        def half(cells):
+            return cells.start // HALF
 
-        def plain_gathers(t, cells):
-            nc.scalar.activation(from_west[:, t - 1, cells], u[t][:].indirect(west_sb[:, entries(cells)]), COPY, scale=-0.5)
-            nc.scalar.activation(from_east[:, t - 1, cells], u[t][:].indirect(east_sb[:, entries(cells)]), COPY, scale=0.5)
+        def local(cells):
+            return slice(cells.start % HALF, (cells.stop - 1) % HALF + 1)
 
-        def differences(t, cells):
-            nc.vector.scalar_tensor_tensor(a[:, t, cells], u[t][:, cells], 0.5, from_west[:, t - 1, cells], ALU.mult, ALU.add)
-            nc.vector.scalar_tensor_tensor(b[:, t, cells], u[t][:, cells], -0.5, from_east[:, t - 1, cells], ALU.mult, ALU.add)
+        def fused_east(cells):
+            nc.vector.tensor_tensor(b[half(cells)][:, 0, :], u[0][:].indirect(east_sb[:, entries(cells)]), v0[:, cells], ALU.add)
+
+        def fused_west(cells):
+            nc.vector.tensor_tensor(a[half(cells)][:, 0, :], v0[:].indirect(west_sb[:, entries(cells)]), u[0][:, cells], ALU.add)
+
+        def early_gathers(t):
+            early_west[t] = sb.tile([P, HALF], F32, name=f"early_west{t}", tag=f"early_west{t}", align_bytes=64)
+            early_east[t] = sb.tile([P, HALF], F32, name=f"early_east{t}", tag=f"early_east{t}", align_bytes=64)
+            nc.scalar.activation(early_west[t][:], u[t][:].indirect(west_sb[:, entries(first)]), COPY, scale=-0.5)
+            nc.scalar.activation(early_east[t][:], u[t][:].indirect(east_sb[:, entries(first)]), COPY, scale=0.5)
+
+        def west_gathers(cells):
+            for t in range(1, PACK):
+                nc.scalar.activation(late_west[:, t - 1, local(cells)], u[t][:].indirect(west_sb[:, entries(cells)]), COPY, scale=-0.5)
+
+        def east_gathers(cells):
+            for t in range(1, PACK):
+                nc.scalar.activation(late_east[:, t - 1, local(cells)], u[t][:].indirect(east_sb[:, entries(cells)]), COPY, scale=0.5)
+
+        def differences(t):
+            nc.vector.scalar_tensor_tensor(a[0][:, t, :], u[t][:, first], 0.5, early_west[t][:], ALU.mult, ALU.add)
+            nc.vector.scalar_tensor_tensor(b[0][:, t, :], u[t][:, first], -0.5, early_east[t][:], ALU.mult, ALU.add)
 
         def west_difference(cells):
-            nc.vector.scalar_tensor_tensor(a[:, 1:, cells], centre[:, 1:, cells], 0.5, from_west[:, :, cells], ALU.mult, ALU.add)
+            nc.vector.scalar_tensor_tensor(a[1][:, 1:, local(cells)], centre[:, 1:, local(cells)], 0.5, late_west[:, :, local(cells)], ALU.mult, ALU.add)
 
         def east_difference(cells):
-            nc.vector.scalar_tensor_tensor(b[:, 1:, cells], centre[:, 1:, cells], -0.5, from_east[:, :, cells], ALU.mult, ALU.add)
+            nc.vector.scalar_tensor_tensor(b[1][:, 1:, local(cells)], centre[:, 1:, local(cells)], -0.5, late_east[:, :, local(cells)], ALU.mult, ALU.add)
 
         def clamp_low(t0, t1, cells):
-            nc.vector.scalar_tensor_tensor(low[:, t0:t1, cells], b[:, t0:t1, cells], 0.0, a[:, t0:t1, cells], ALU.min, ALU.max)
+            h, c = half(cells), local(cells)
+            nc.vector.scalar_tensor_tensor(low[:, t0:t1, cells], b[h][:, t0:t1, c], 0.0, a[h][:, t0:t1, c], ALU.min, ALU.max)
 
         def clamp_high(t0, t1, cells):
-            nc.vector.scalar_tensor_tensor(slope[:, t0:t1, cells], b[:, t0:t1, cells], 0.0, low[:, t0:t1, cells], ALU.max, ALU.min)
+            h, c = half(cells), local(cells)
+            nc.vector.scalar_tensor_tensor(slope[:, t0:t1, cells], b[h][:, t0:t1, c], 0.0, low[:, t0:t1, cells], ALU.max, ALU.min)
 
         z_bf = {}
         z_codes = {}
@@ -173,8 +198,39 @@ def tile_picked_minmod_none_p_kernel(tc, x_words, x_scales, w1, gn, w2, offs, ea
             nc.vector.tensor_tensor(
                 z_bf[cells.start][:].rearrange("p (c i t) -> p c t i", i=2, t=PACK),
                 slope[:, :, cells].rearrange("p t (c i) -> p c t i", i=2),
-                centre[:, :, cells].rearrange("p t (c i) -> p c t i", i=2),
+                centre[:, :, local(cells)].rearrange("p t (c i) -> p c t i", i=2),
                 ALU.add,
+            )
+
+        zt = {}
+
+        def open_sum(r):
+            zt[r] = psum.tile([P, PACK, P], F32, name=f"zt{r}", tag=f"bank{5 + r}")
+            terms = [0, 0, 1, 2, 3]
+            for i, t in enumerate(terms):
+                nc.tensor.matmul(zt[r][:, t, :], u[t][:, r * P : (r + 1) * P], ident[:], start=(i == 0), stop=False, is_transpose=True)
+
+        def add_slope(r, t0, t1):
+            for t in range(t0, t1):
+                nc.tensor.matmul(zt[r][:, t, :], slope[:, t, r * P : (r + 1) * P], ident[:], start=False, stop=(t == PACK - 1), is_transpose=True)
+
+        pairs = {}
+
+        def round_sum(r):
+            rounded = sb.tile([P, PACK * P], BF16, name=f"rounded{r}", align_bytes=64)
+            nc.scalar.copy(
+                rounded[:].rearrange("c (e p k) -> c e p k", e=2, k=2),
+                zt[r][:].rearrange("c (e k) p -> c e p k", k=2),
+            )
+            pairs[r] = psum.tile([P, 2, P], F32, name=f"pairs{r}", tag=f"bank{(7, 3)[r]}")
+            for e in range(2):
+                nc.tensor.transpose(pairs[r][:, e, :], rounded[:].bitcast(F32)[:, e * P : (e + 1) * P], ident[:])
+
+        def turn_back(r):
+            z_bf[r * P] = sb.tile([P, PACK * P], BF16, name=f"z_bf{r * P}", align_bytes=64)
+            nc.scalar.copy(
+                z_bf[r * P][:].bitcast(F32).rearrange("p (c e) -> p c e", e=2),
+                pairs[r][:].rearrange("p e c -> p c e"),
             )
 
         def quantize_z(cells):
@@ -192,7 +248,7 @@ def tile_picked_minmod_none_p_kernel(tc, x_words, x_scales, w1, gn, w2, offs, ea
                 nc.tensor.matmul_mx(
                     out=acc[:, g - g0, :],
                     lhsT=w2_codes[:, rows].bitcast(FP8X4),
-                    lhsT_scale=w2_scales[:, rows],
+                    lhsT_scale=w2_scales[g // 2][:, g % 2 * P : (g % 2 + 1) * P],
                     rhs=z_codes[cells.start][:].bitcast(FP8X4),
                     rhs_scale=z_scales[cells.start][:],
                     start=True,
@@ -201,50 +257,63 @@ def tile_picked_minmod_none_p_kernel(tc, x_words, x_scales, w1, gn, w2, offs, ea
             copy(res[:], acc[:])
             nc.sync.dma_start(out[g0 * P : g1 * P, cells].rearrange("(g p) n -> p g n", p=P), res[:])
 
-        first = slice(0, 256)
-        second = slice(256, 512)
-        third_block = slice(256, 384)
-        last_block = slice(384, 512)
+        first = slice(0, HALF)
+        second = slice(HALF, S)
+        block = [slice(r * P, (r + 1) * P) for r in range(4)]
 
         leave(1)
         leave(2)
-        fused_gathers(first)
-        plain_gathers(1, first)
+        fused_east(first)
+        nc.vector.tensor_scalar(v0[:, second], u[0][:, second], -1.0, None, ALU.mult)
+        fused_east(second)
+        fused_west(first)
+        quantize_w2(0, "w2_scales0")
+        early_gathers(1)
         leave(3)
-        fused_gathers(second)
-        plain_gathers(2, first)
-        plain_gathers(3, first)
-        nc.vector.tensor_scalar(centre[:, 0, :], u[0][:], 2.0, None, ALU.mult)
-        differences(1, first)
-        quantize_w2(0)
+        early_gathers(2)
+        early_gathers(3)
+        west_gathers(second)
+        east_gathers(block[2])
+        east_gathers(block[3])
+        open_sum(0)
+        open_sum(1)
+        differences(1)
+        quantize_w2(1, "early_west1")
         clamp_low(0, 2, first)
-        differences(2, first)
-        round_w2(1, nc.scalar.copy)
+        differences(2)
+        centre = sb.tile([P, PACK, HALF], F32, name="centre", tag="early_west2", align_bytes=64)
         for t in range(1, PACK):
-            plain_gathers(t, third_block)
-        for t in range(1, PACK):
-            plain_gathers(t, last_block)
+            nc.sync.dma_start(centre[:, t, :], u[t][:, second])
         clamp_high(0, 2, first)
-        differences(3, first)
-        quantize_w2(1)
+        add_slope(0, 0, 2)
+        add_slope(1, 0, 2)
+        differences(3)
+        nc.vector.tensor_scalar(centre[:, 0, :], u[0][:, second], 2.0, None, ALU.mult)
         clamp_low(2, 4, first)
-        west_difference(third_block)
+        a[1] = sb.tile([P, PACK, HALF], F32, name="a1", tag="early_east1", align_bytes=64)
+        fused_west(second)
         clamp_high(2, 4, first)
-        east_difference(third_block)
-        add_centre(first)
-        clamp_low(0, 4, third_block)
-        quantize_z(first)
-        second_product(first, 0, 2, 5, nc.scalar.copy)
-        second_product(first, 2, 4, 6, nc.scalar.copy)
-        clamp_high(0, 4, third_block)
-        west_difference(last_block)
-        add_centre(third_block)
-        east_difference(last_block)
-        quantize_z(third_block)
-        second_product(third_block, 0, 4, 7, nc.scalar.copy)
-        clamp_low(0, 4, last_block)
-        clamp_high(0, 4, last_block)
-        add_centre(last_block)
-        quantize_z(last_block)
-        second_product(last_block, 0, 2, 0, nc.scalar.copy)
-        second_product(last_block, 2, 4, 1, nc.vector.tensor_copy)
+        add_slope(0, 2, 4)
+        add_slope(1, 2, 4)
+        round_sum(0)
+        round_sum(1)
+        turn_back(0)
+        turn_back(1)
+        west_difference(second)
+        east_difference(block[2])
+        east_difference(block[3])
+        clamp_low(0, 4, block[2])
+        clamp_low(0, 4, block[3])
+        clamp_high(0, 4, block[2])
+        quantize_z(block[0])
+        second_product(block[0], 0, 4, 1, nc.scalar.copy)
+        quantize_z(block[1])
+        second_product(block[1], 0, 4, 2, nc.scalar.copy)
+        add_centre(block[2])
+        clamp_high(0, 4, block[3])
+        quantize_z(block[2])
+        second_product(block[2], 0, 4, 5, nc.scalar.copy)
+        add_centre(block[3])
+        quantize_z(block[3])
+        second_product(block[3], 0, 2, 0, nc.scalar.copy)
+        second_product(block[3], 2, 4, 4, nc.vector.tensor_copy)

@@ -19,103 +19,106 @@ COPY = mybir.ActivationFunctionType.Copy
 P = 128
 PACK = 4
 HALF = S // 2
-M_VECTOR = 60
-W2_SCALAR = 36
+W1_VECTOR = 40
+W2_HALF_BYTES = 4 * PACK * HALF
 
 
 def tile_picked_minmod_none_p_kernel(tc, x_words, x_scales, w1, gn, w2, offs, east, west, out):
     nc = tc.nc
     with ExitStack() as ctx:
         sb = ctx.enter_context(tc.tile_pool(name="sb", bufs=1))
-        late = ctx.enter_context(tc.tile_pool(name="late", bufs=1))
+        shared = ctx.enter_context(tc.tile_pool(name="shared", bufs=1))
         psum = ctx.enter_context(tc.psum_pool(name="psum", bufs=1))
 
         offs_sb = sb.tile([P, S // 16], U16, name="offs_sb")
         east_sb = sb.tile([P, S // 16], U16, name="east_sb")
         west_sb = sb.tile([P, S // 16], U16, name="west_sb")
-        xs = sb.tile([P, T], U8, name="xs", tag="xs", align_bytes=64)
-        w1_raw = sb.tile([P, PACK, H], F32, name="w1_raw", tag="w_raw", align_bytes=64)
-        gn_sb = late.tile([P, 32], F32, name="gn_sb", offset=4 * T - 64, align_bytes=64)
+        xs = shared.tile([P, T], U8, name="xs", offset=W2_HALF_BYTES - T // 2, align_bytes=64)
+        xw = sb.tile([P, T], U32, name="xw", align_bytes=64)
+        w1_raw = [sb.tile([P, PACK, HALF], F32, name=f"w1_raw{h}", align_bytes=64) for h in range(2)]
         gain = sb.tile([P, PACK], F32, name="gain")
         g_pos = sb.tile([P, 1], F32, name="g_pos")
         g_neg = sb.tile([P, 1], F32, name="g_neg")
         ident = sb.tile([P, P], F32, name="ident", align_bytes=64)
+        spread_scales = sb.tile([P, S], U8, name="spread_scales", align_bytes=64)
+        xg_scales = sb.tile([P, S], U8, name="xg_scales", align_bytes=64)
 
-        nc.vector.memset(xs[:].bitcast(I32), 0)
-        nc.scalar.dma_start(gn_sb[:, :PACK], gn.rearrange("(p t) o -> p (t o)", t=PACK))
         nc.sync.dma_start(offs_sb[:], offs)
-        nc.sync.dma_start(w1_raw[:], w1.rearrange("(p j) c -> p j c", j=PACK))
+        nc.scalar.dma_start(gain[:], gn.rearrange("(p t) o -> p (t o)", t=PACK))
+        nc.sync.dma_start(xs[0:32, :].bitcast(I32), x_scales[0].bitcast(I32).unsqueeze(1).to_broadcast([16, 2, T // 4]))
+        nc.vector.memset(xs[32:64, :].bitcast(I32), 0)
+        nc.vector.memset(xs[64:128, :].bitcast(I32), 0)
+        nc.vector.memset(xg_scales[:].bitcast(I32), 0)
+        nc.sync.dma_start(xw[:].bitcast(I32), x_words[0].rearrange("p n t -> p (n t)").bitcast(I32))
         nc.sync.dma_start(east_sb[:], east)
+        for h in range(2):
+            nc.sync.dma_start(w1_raw[h][:], w1[:, h * HALF : (h + 1) * HALF].rearrange("(p j) c -> p j c", j=PACK))
         nc.sync.dma_start(west_sb[:], west)
-        for q in range(4):
-            nc.sync.dma_start(xs[32 * q : 32 * q + 4, :].bitcast(I32), x_scales[0, 4 * q : 4 * q + 4, :].bitcast(I32))
-        nc.vector.tensor_copy(gain[:], gn_sb[:, :PACK])
+        make_identity(nc, ident[:])
         nc.vector.tensor_scalar(g_pos[:], gain[:, 0:1], 0.5, None, ALU.mult)
         nc.vector.tensor_scalar(g_neg[:], gain[:, 0:1], -0.5, None, ALU.mult)
-        xw = late.tile([P, T], U32, name="xw", offset=0, align_bytes=64)
-        nc.sync.dma_start(xw[:].bitcast(I32), x_words[0].rearrange("p n t -> p (n t)").bitcast(I32))
-        make_identity(nc, ident[:])
 
-        w1_bf = sb.tile([P, PACK * H], BF16, name="w1_bf", align_bytes=64)
-        w1_dst = w1_bf[:].rearrange("p (t m j) -> p m t j", t=PACK, j=PACK)
-        w1_src = w1_raw[:].rearrange("p j (m t) -> p m t j", t=PACK)
-        nc.vector.tensor_copy(w1_dst[:, :M_VECTOR], w1_src[:, :M_VECTOR])
-        nc.scalar.activation(w1_dst[:, M_VECTOR:], w1_src[:, M_VECTOR:], COPY)
+        nc.vector.tensor_copy(spread_scales[:], xs[:].indirect(offs_sb[:]))
+        for q in range(4):
+            nc.sync.dma_start(xg_scales[32 * q : 32 * q + 4, :].bitcast(I32), spread_scales[8 * q : 8 * q + 8 : 2, :].bitcast(I32))
 
-        w2_raw = late.tile([P, 2, PACK, N // 2], F32, name="w2_raw", offset=4 * T, align_bytes=64)
+        w2_raw = [shared.tile([P, PACK, HALF], F32, name=f"w2_raw{h}", offset=h * W2_HALF_BYTES, align_bytes=64) for h in range(2)]
         for h in range(2):
-            nc.sync.dma_start(w2_raw[:, h], w2[:, h * HALF : (h + 1) * HALF].rearrange("(p j) c -> p j c", j=PACK))
-
-        xg_scales = sb.tile([P, S], U8, name="xg_scales", align_bytes=64)
-        nc.vector.tensor_copy(xg_scales[:], xs[:].indirect(offs_sb[:]))
-
-        w1_codes = {}
-        w1_scales = {}
-
-        def quantize_w1(t0, t1, scales):
-            codes = sb.tile([P, (t1 - t0) * P], U32, name=f"w1_codes{t0}", align_bytes=64)
-            nc.vector.quantize_mx(out=codes[:].bitcast(FP8X4), scales=scales[:], in_=w1_bf[:, t0 * H : t1 * H])
-            for t in range(t0, t1):
-                w1_codes[t] = codes[:, (t - t0) * P : (t - t0 + 1) * P]
-                w1_scales[t] = scales[:, (t - t0) * P : (t - t0 + 1) * P]
-
-        quantize_w1(0, 2, sb.tile([P, 2 * P], U8, name="w1_scales0", tag="xs", align_bytes=64))
+            nc.sync.dma_start(w2_raw[h][:], w2[:, h * HALF : (h + 1) * HALF].rearrange("(p j) c -> p j c", j=PACK))
 
         xg = sb.tile([P, S], U32, name="xg", align_bytes=64)
+        nc.vector.tensor_copy(xg[:], xw[:].indirect(offs_sb[:]))
+
+        w1_bf = sb.tile([P, PACK, 2, HALF], BF16, name="w1_bf", align_bytes=64)
+        w1_codes = sb.tile([P, PACK, P], U32, name="w1_codes", align_bytes=64)
+        w1_scales = sb.tile([P, PACK, P], U8, name="w1_scales", align_bytes=64)
+
+        def round_w1(h, m0, m1, copy):
+            copy(
+                w1_bf[:, :, h, :].rearrange("p t (m j) -> p m t j", j=PACK)[:, m0:m1],
+                w1_raw[h][:].rearrange("p j (m t) -> p m t j", t=PACK)[:, m0:m1],
+            )
+
+        def quantize_w1(h, t):
+            cols = slice(64 * h, 64 * h + 64)
+            nc.vector.quantize_mx(out=w1_codes[:, t, cols].bitcast(FP8X4), scales=w1_scales[:, t, cols], in_=w1_bf[:, t, h, :])
+
         for h in range(2):
-            nc.vector.tensor_copy(xg[:, h * HALF : (h + 1) * HALF], xw[:].indirect(offs_sb[:, 16 * h : 16 * h + 16]))
-        quantize_w1(2, 4, late.tile([P, 2 * P], U8, name="w1_scales2", offset=0, align_bytes=64))
+            round_w1(h, 0, W1_VECTOR, nc.vector.tensor_copy)
+            round_w1(h, W1_VECTOR, 64, nc.scalar.copy)
+            for t in range(PACK):
+                quantize_w1(h, t)
 
         u = [sb.tile([P, S], F32, name=f"u{t}", align_bytes=64) for t in range(PACK)]
-        v0 = sb.tile([P, S], F32, name="v0", align_bytes=64)
 
         def first_product(acc, t, cols):
             nc.tensor.matmul_mx(
                 out=acc,
-                lhsT=w1_codes[t].bitcast(FP8X4),
-                lhsT_scale=w1_scales[t],
+                lhsT=w1_codes[:, t, :].bitcast(FP8X4),
+                lhsT_scale=w1_scales[:, t, :],
                 rhs=xg[:, cols].bitcast(FP8X4),
                 rhs_scale=xg_scales[:, cols],
                 start=True,
                 stop=True,
             )
 
-        w2_bf = [sb.tile([P, PACK * HALF], BF16, name=f"w2_bf{h}", align_bytes=64) for h in range(2)]
+        w2_bf = {}
         w2_codes = sb.tile([P, N], U32, name="w2_codes", align_bytes=64)
         w2_scales = {}
 
-        def round_w2(h, c0, c1, copy):
-            copy(
-                w2_bf[h][:].rearrange("p (c i j) -> p c j i", i=4, j=PACK)[:, c0:c1],
-                w2_raw[:, h].rearrange("p j (c i) -> p c j i", i=4)[:, c0:c1],
+        def round_w2(h, tag):
+            w2_bf[h] = sb.tile([P, PACK * HALF], BF16, name=f"w2_bf{h}", tag=tag, align_bytes=64)
+            nc.vector.tensor_copy(
+                w2_bf[h][:].rearrange("p (c i j) -> p c j i", i=4, j=PACK),
+                w2_raw[h][:].rearrange("p j (c i) -> p c j i", i=4),
             )
 
         def quantize_w2(h, tag):
             w2_scales[h] = sb.tile([P, HALF], U8, name=f"w2_scales{h}", tag=tag, align_bytes=64)
             nc.vector.quantize_mx(out=w2_codes[:, h * HALF : (h + 1) * HALF].bitcast(FP8X4), scales=w2_scales[h][:], in_=w2_bf[h][:])
 
-        round_w2(0, 0, W2_SCALAR, nc.scalar.copy)
-        round_w2(0, W2_SCALAR, 64, nc.vector.tensor_copy)
+        round_w2(0, "w2_bf0")
+        v0 = shared.tile([P, S], F32, name="v0", offset=0, align_bytes=64)
 
         for h in range(2):
             acc = psum.tile([P, HALF], F32, name=f"y0{h}", tag=f"bank{h}")
@@ -124,8 +127,6 @@ def tile_picked_minmod_none_p_kernel(tc, x_words, x_scales, w1, gn, w2, offs, ea
             nc.scalar.activation(u[0][:, cols], acc[:], COPY, scale=g_pos[:])
             if h == 0:
                 nc.vector.tensor_scalar(v0[:, cols], acc[:], g_neg[:], None, ALU.mult)
-
-        round_w2(1, 0, 64, nc.vector.tensor_copy)
 
         def leave(t):
             acc = psum.tile([P, S], F32, name=f"y{t}", tag=f"bank{t + 1}")
@@ -267,7 +268,6 @@ def tile_picked_minmod_none_p_kernel(tc, x_words, x_scales, w1, gn, w2, offs, ea
         nc.vector.tensor_scalar(v0[:, second], u[0][:, second], -1.0, None, ALU.mult)
         fused_east(second)
         fused_west(first)
-        quantize_w2(0, "w2_scales0")
         early_gathers(1)
         leave(3)
         early_gathers(2)
@@ -278,19 +278,21 @@ def tile_picked_minmod_none_p_kernel(tc, x_words, x_scales, w1, gn, w2, offs, ea
         open_sum(0)
         open_sum(1)
         differences(1)
-        quantize_w2(1, "early_west1")
+        quantize_w2(0, "early_west1")
         clamp_low(0, 2, first)
+        round_w2(1, "early_east1")
         differences(2)
-        centre = sb.tile([P, PACK, HALF], F32, name="centre", tag="early_west2", align_bytes=64)
+        centre = sb.tile([P, PACK, HALF], F32, name="centre", align_bytes=64)
         for t in range(1, PACK):
             nc.sync.dma_start(centre[:, t, :], u[t][:, second])
         clamp_high(0, 2, first)
         add_slope(0, 0, 2)
         add_slope(1, 0, 2)
         differences(3)
+        quantize_w2(1, "w2_scales1")
         nc.vector.tensor_scalar(centre[:, 0, :], u[0][:, second], 2.0, None, ALU.mult)
         clamp_low(2, 4, first)
-        a[1] = sb.tile([P, PACK, HALF], F32, name="a1", tag="early_east1", align_bytes=64)
+        a[1] = sb.tile([P, PACK, HALF], F32, name="a1", tag="early_east2", align_bytes=64)
         fused_west(second)
         clamp_high(2, 4, first)
         add_slope(0, 2, 4)

@@ -19,7 +19,7 @@ COPY = mybir.ActivationFunctionType.Copy
 P = 128
 PACK = 4
 HALF = S // 2
-W1_VECTOR = 40
+W1_VECTOR = 84
 W2_HALF_BYTES = 4 * PACK * HALF
 
 
@@ -35,7 +35,7 @@ def tile_picked_minmod_none_p_kernel(tc, x_words, x_scales, w1, gn, w2, offs, ea
         west_sb = sb.tile([P, S // 16], U16, name="west_sb")
         xs = shared.tile([P, T], U8, name="xs", offset=W2_HALF_BYTES - T // 2, align_bytes=64)
         xw = sb.tile([P, T], U32, name="xw", align_bytes=64)
-        w1_raw = [sb.tile([P, PACK, HALF], F32, name=f"w1_raw{h}", align_bytes=64) for h in range(2)]
+        w1_raw = sb.tile([P, PACK, H], F32, name="w1_raw", align_bytes=64)
         gain = sb.tile([P, PACK], F32, name="gain")
         g_pos = sb.tile([P, 1], F32, name="g_pos")
         g_neg = sb.tile([P, 1], F32, name="g_neg")
@@ -49,10 +49,9 @@ def tile_picked_minmod_none_p_kernel(tc, x_words, x_scales, w1, gn, w2, offs, ea
         nc.vector.memset(xs[32:64, :].bitcast(I32), 0)
         nc.vector.memset(xs[64:128, :].bitcast(I32), 0)
         nc.vector.memset(xg_scales[:].bitcast(I32), 0)
-        nc.sync.dma_start(xw[:].bitcast(I32), x_words[0].rearrange("p n t -> p (n t)").bitcast(I32))
+        nc.sync.dma_start(w1_raw[:], w1.rearrange("(p j) c -> p j c", j=PACK))
         nc.sync.dma_start(east_sb[:], east)
-        for h in range(2):
-            nc.sync.dma_start(w1_raw[h][:], w1[:, h * HALF : (h + 1) * HALF].rearrange("(p j) c -> p j c", j=PACK))
+        nc.sync.dma_start(xw[:].bitcast(I32), x_words[0].rearrange("p n t -> p (n t)").bitcast(I32))
         nc.sync.dma_start(west_sb[:], west)
         make_identity(nc, ident[:])
         nc.vector.tensor_scalar(g_pos[:], gain[:, 0:1], 0.5, None, ALU.mult)
@@ -66,28 +65,22 @@ def tile_picked_minmod_none_p_kernel(tc, x_words, x_scales, w1, gn, w2, offs, ea
         for h in range(2):
             nc.sync.dma_start(w2_raw[h][:], w2[:, h * HALF : (h + 1) * HALF].rearrange("(p j) c -> p j c", j=PACK))
 
-        xg = sb.tile([P, S], U32, name="xg", align_bytes=64)
-        nc.vector.tensor_copy(xg[:], xw[:].indirect(offs_sb[:]))
-
-        w1_bf = sb.tile([P, PACK, 2, HALF], BF16, name="w1_bf", align_bytes=64)
+        w1_bf = sb.tile([P, PACK * H], BF16, name="w1_bf", align_bytes=64)
         w1_codes = sb.tile([P, PACK, P], U32, name="w1_codes", align_bytes=64)
         w1_scales = sb.tile([P, PACK, P], U8, name="w1_scales", align_bytes=64)
+        w1_dst = w1_bf[:].rearrange("p (t m j) -> p m t j", t=PACK, j=PACK)
+        w1_src = w1_raw[:].rearrange("p j (m t) -> p m t j", t=PACK)
+        nc.vector.tensor_copy(w1_dst[:, :W1_VECTOR], w1_src[:, :W1_VECTOR])
+        nc.scalar.copy(w1_dst[:, W1_VECTOR:], w1_src[:, W1_VECTOR:])
+        nc.vector.quantize_mx(
+            out=w1_codes[:].rearrange("p t m -> p (t m)").bitcast(FP8X4),
+            scales=w1_scales[:].rearrange("p t m -> p (t m)"),
+            in_=w1_bf[:],
+        )
 
-        def round_w1(h, m0, m1, copy):
-            copy(
-                w1_bf[:, :, h, :].rearrange("p t (m j) -> p m t j", j=PACK)[:, m0:m1],
-                w1_raw[h][:].rearrange("p j (m t) -> p m t j", t=PACK)[:, m0:m1],
-            )
-
-        def quantize_w1(h, t):
-            cols = slice(64 * h, 64 * h + 64)
-            nc.vector.quantize_mx(out=w1_codes[:, t, cols].bitcast(FP8X4), scales=w1_scales[:, t, cols], in_=w1_bf[:, t, h, :])
-
+        xg = sb.tile([P, S], U32, name="xg", align_bytes=64)
         for h in range(2):
-            round_w1(h, 0, W1_VECTOR, nc.vector.tensor_copy)
-            round_w1(h, W1_VECTOR, 64, nc.scalar.copy)
-            for t in range(PACK):
-                quantize_w1(h, t)
+            nc.vector.tensor_copy(xg[:, h * HALF : (h + 1) * HALF], xw[:].indirect(offs_sb[:, 16 * h : 16 * h + 16]))
 
         u = [sb.tile([P, S], F32, name=f"u{t}", align_bytes=64) for t in range(PACK)]
 
@@ -127,6 +120,8 @@ def tile_picked_minmod_none_p_kernel(tc, x_words, x_scales, w1, gn, w2, offs, ea
             nc.scalar.activation(u[0][:, cols], acc[:], COPY, scale=g_pos[:])
             if h == 0:
                 nc.vector.tensor_scalar(v0[:, cols], acc[:], g_neg[:], None, ALU.mult)
+
+        round_w2(1, "w2_bf1")
 
         def leave(t):
             acc = psum.tile([P, S], F32, name=f"y{t}", tag=f"bank{t + 1}")
@@ -280,7 +275,6 @@ def tile_picked_minmod_none_p_kernel(tc, x_words, x_scales, w1, gn, w2, offs, ea
         differences(1)
         quantize_w2(0, "early_west1")
         clamp_low(0, 2, first)
-        round_w2(1, "early_east1")
         differences(2)
         centre = sb.tile([P, PACK, HALF], F32, name="centre", align_bytes=64)
         for t in range(1, PACK):
@@ -289,14 +283,14 @@ def tile_picked_minmod_none_p_kernel(tc, x_words, x_scales, w1, gn, w2, offs, ea
         add_slope(0, 0, 2)
         add_slope(1, 0, 2)
         differences(3)
-        quantize_w2(1, "w2_scales1")
-        nc.vector.tensor_scalar(centre[:, 0, :], u[0][:, second], 2.0, None, ALU.mult)
+        quantize_w2(1, "early_east2")
         clamp_low(2, 4, first)
-        a[1] = sb.tile([P, PACK, HALF], F32, name="a1", tag="early_east2", align_bytes=64)
+        a[1] = sb.tile([P, PACK, HALF], F32, name="a1", tag="early_east1", align_bytes=64)
         fused_west(second)
         clamp_high(2, 4, first)
         add_slope(0, 2, 4)
         add_slope(1, 2, 4)
+        nc.scalar.activation(centre[:, 0, :], u[0][:, second], COPY, scale=2.0)
         round_sum(0)
         round_sum(1)
         turn_back(0)

@@ -263,6 +263,7 @@ def tile_picked_minmod_none_p_kernel(tc, x_words, x_scales, w1, gn, w2, offs, ea
         nc.vector.tensor_scalar(v0[:, second], u[0][:, second], -1.0, None, ALU.mult)
         fused_east(second)
         fused_west(first)
+        quantize_w2(0, "w2_scales0")
         early_gathers(1)
         leave(3)
         early_gathers(2)
@@ -273,24 +274,23 @@ def tile_picked_minmod_none_p_kernel(tc, x_words, x_scales, w1, gn, w2, offs, ea
         open_sum(0)
         open_sum(1)
         differences(1)
-        quantize_w2(0, "early_west1")
+        quantize_w2(1, "early_west1")
         clamp_low(0, 2, first)
         differences(2)
-        centre = sb.tile([P, PACK, HALF], F32, name="centre", align_bytes=64)
+        centre = sb.tile([P, PACK, HALF], F32, name="centre", tag="early_west2", align_bytes=64)
         for t in range(1, PACK):
             nc.sync.dma_start(centre[:, t, :], u[t][:, second])
         clamp_high(0, 2, first)
         add_slope(0, 0, 2)
         add_slope(1, 0, 2)
         differences(3)
-        quantize_w2(1, "early_east2")
+        nc.vector.tensor_scalar(centre[:, 0, :], u[0][:, second], 2.0, None, ALU.mult)
         clamp_low(2, 4, first)
         a[1] = sb.tile([P, PACK, HALF], F32, name="a1", tag="early_east1", align_bytes=64)
         fused_west(second)
         clamp_high(2, 4, first)
         add_slope(0, 2, 4)
         add_slope(1, 2, 4)
-        nc.scalar.activation(centre[:, 0, :], u[0][:, second], COPY, scale=2.0)
         round_sum(0)
         round_sum(1)
         turn_back(0)

@@ -120,8 +120,9 @@ def tile_picked_minmod_none_p_kernel(tc, x_words, x_scales, w1, gn, w2, offs, ea
             nc.scalar.activation(u[0][:, cols], acc[:], COPY, scale=g_pos[:])
             if h == 0:
                 nc.vector.tensor_scalar(v0[:, cols], acc[:], g_neg[:], None, ALU.mult)
-
-        round_w2(1, "w2_bf1")
+            acc = psum.tile([P, HALF], F32, name=f"y1{h}", tag=f"bank{(2, 7)[h]}")
+            first_product(acc[:], 1, cols)
+            nc.scalar.activation(u[1][:, cols], acc[:], COPY, scale=gain[:, 1:2])
 
         def leave(t):
             acc = psum.tile([P, S], F32, name=f"y{t}", tag=f"bank{t + 1}")
@@ -162,8 +163,8 @@ def tile_picked_minmod_none_p_kernel(tc, x_words, x_scales, w1, gn, w2, offs, ea
             for t in range(1, PACK):
                 nc.scalar.activation(late_west[:, t - 1, local(cells)], u[t][:].indirect(west_sb[:, entries(cells)]), COPY, scale=-0.5)
 
-        def east_gathers(cells):
-            for t in range(1, PACK):
+        def east_gathers(cells, t1):
+            for t in range(1, t1):
                 nc.scalar.activation(late_east[:, t - 1, local(cells)], u[t][:].indirect(east_sb[:, entries(cells)]), COPY, scale=0.5)
 
         def differences(t):
@@ -188,15 +189,17 @@ def tile_picked_minmod_none_p_kernel(tc, x_words, x_scales, w1, gn, w2, offs, ea
         z_codes = {}
         z_scales = {}
 
-        def add_centre(cells):
-            width = cells.stop - cells.start
-            z_bf[cells.start] = sb.tile([P, PACK * width], BF16, name=f"z_bf{cells.start}", align_bytes=64)
-            nc.vector.tensor_tensor(
-                z_bf[cells.start][:].rearrange("p (c i t) -> p c t i", i=2, t=PACK),
-                slope[:, :, cells].rearrange("p t (c i) -> p c t i", i=2),
-                centre[:, :, local(cells)].rearrange("p t (c i) -> p c t i", i=2),
-                ALU.add,
-            )
+        def add_centre(cells, parts):
+            width = (cells.stop - cells.start) // parts
+            z_bf[cells.start] = sb.tile([P, parts, PACK * width], BF16, name=f"z_bf{cells.start}", align_bytes=64)
+            for part in range(parts):
+                some = slice(cells.start + part * width, cells.start + (part + 1) * width)
+                nc.vector.tensor_tensor(
+                    z_bf[cells.start][:, part, :].rearrange("p (c i t) -> p c t i", i=2, t=PACK),
+                    slope[:, :, some].rearrange("p t (c i) -> p c t i", i=2),
+                    centre[:, :, local(some)].rearrange("p t (c i) -> p c t i", i=2),
+                    ALU.add,
+                )
 
         zt = {}
 
@@ -223,17 +226,19 @@ def tile_picked_minmod_none_p_kernel(tc, x_words, x_scales, w1, gn, w2, offs, ea
                 nc.tensor.transpose(pairs[r][:, e, :], rounded[:].bitcast(F32)[:, e * P : (e + 1) * P], ident[:])
 
         def turn_back(r):
-            z_bf[r * P] = sb.tile([P, PACK * P], BF16, name=f"z_bf{r * P}", align_bytes=64)
+            z_bf[r * P] = sb.tile([P, 1, PACK * P], BF16, name=f"z_bf{r * P}", align_bytes=64)
             nc.scalar.copy(
-                z_bf[r * P][:].bitcast(F32).rearrange("p (c e) -> p c e", e=2),
+                z_bf[r * P][:, 0, :].bitcast(F32).rearrange("p (c e) -> p c e", e=2),
                 pairs[r][:].rearrange("p e c -> p c e"),
             )
 
-        def quantize_z(cells):
+        def quantize_z(cells, parts=1):
             width = cells.stop - cells.start
             z_codes[cells.start] = sb.tile([P, width], U32, name=f"z_codes{cells.start}", align_bytes=64)
             z_scales[cells.start] = sb.tile([P, width], U8, name=f"z_scales{cells.start}", align_bytes=64)
-            nc.vector.quantize_mx(out=z_codes[cells.start][:].bitcast(FP8X4), scales=z_scales[cells.start][:], in_=z_bf[cells.start][:])
+            for part in range(parts):
+                cols = slice(part * width // parts, (part + 1) * width // parts)
+                nc.vector.quantize_mx(out=z_codes[cells.start][:, cols].bitcast(FP8X4), scales=z_scales[cells.start][:, cols], in_=z_bf[cells.start][:, part, :])
 
         def second_product(cells, g0, g1, bank, copy):
             width = cells.stop - cells.start
@@ -257,7 +262,6 @@ def tile_picked_minmod_none_p_kernel(tc, x_words, x_scales, w1, gn, w2, offs, ea
         second = slice(HALF, S)
         block = [slice(r * P, (r + 1) * P) for r in range(4)]
 
-        leave(1)
         leave(2)
         fused_east(first)
         nc.vector.tensor_scalar(v0[:, second], u[0][:, second], -1.0, None, ALU.mult)
@@ -269,12 +273,12 @@ def tile_picked_minmod_none_p_kernel(tc, x_words, x_scales, w1, gn, w2, offs, ea
         early_gathers(2)
         early_gathers(3)
         west_gathers(second)
-        east_gathers(block[2])
-        east_gathers(block[3])
+        east_gathers(block[2], PACK)
+        east_gathers(block[3], PACK - 1)
         open_sum(0)
         open_sum(1)
         differences(1)
-        quantize_w2(1, "early_west1")
+        round_w2(1, "early_west1")
         clamp_low(0, 2, first)
         differences(2)
         centre = sb.tile([P, PACK, HALF], F32, name="centre", tag="early_west2", align_bytes=64)
@@ -297,19 +301,24 @@ def tile_picked_minmod_none_p_kernel(tc, x_words, x_scales, w1, gn, w2, offs, ea
         turn_back(1)
         west_difference(second)
         east_difference(block[2])
-        east_difference(block[3])
+        quantize_w2(1, "early_east3")
+        nc.vector.tensor_scalar(late_east[:, PACK - 2, P:], u[3][:].indirect(east_sb[:, entries(block[3])]), 0.5, 0.0, ALU.mult, ALU.add)
         clamp_low(0, 4, block[2])
-        clamp_low(0, 4, block[3])
+        east_difference(block[3])
         clamp_high(0, 4, block[2])
+        clamp_low(0, 4, block[3])
         quantize_z(block[0])
-        second_product(block[0], 0, 4, 1, nc.scalar.copy)
+        second_product(block[0], 0, 2, 1, nc.scalar.copy)
+        second_product(block[0], 2, 4, 2, nc.scalar.copy)
+        add_centre(block[2], 1)
         quantize_z(block[1])
-        second_product(block[1], 0, 4, 2, nc.scalar.copy)
-        add_centre(block[2])
+        second_product(block[1], 0, 2, 7, nc.scalar.copy)
+        second_product(block[1], 2, 4, 3, nc.scalar.copy)
         clamp_high(0, 4, block[3])
         quantize_z(block[2])
-        second_product(block[2], 0, 4, 5, nc.scalar.copy)
-        add_centre(block[3])
-        quantize_z(block[3])
+        second_product(block[2], 0, 2, 5, nc.scalar.copy)
+        second_product(block[2], 2, 4, 6, nc.scalar.copy)
+        add_centre(block[3], 2)
+        quantize_z(block[3], 2)
         second_product(block[3], 0, 2, 0, nc.scalar.copy)
         second_product(block[3], 2, 4, 4, nc.vector.tensor_copy)

@@ -274,7 +274,7 @@ def tile_picked_minmod_none_p_kernel(tc, x_words, x_scales, w1, gn, w2, offs, ea
         early_gathers(3)
         west_gathers(second)
         east_gathers(block[2], PACK)
-        east_gathers(block[3], PACK - 1)
+        east_gathers(block[3], PACK)
         open_sum(0)
         open_sum(1)
         differences(1)
@@ -288,7 +288,7 @@ def tile_picked_minmod_none_p_kernel(tc, x_words, x_scales, w1, gn, w2, offs, ea
         add_slope(0, 0, 2)
         add_slope(1, 0, 2)
         differences(3)
-        nc.vector.tensor_scalar(centre[:, 0, :], u[0][:, second], 2.0, None, ALU.mult)
+        quantize_w2(1, "early_west3")
         clamp_low(2, 4, first)
         a[1] = sb.tile([P, PACK, HALF], F32, name="a1", tag="early_east1", align_bytes=64)
         fused_west(second)
@@ -301,8 +301,7 @@ def tile_picked_minmod_none_p_kernel(tc, x_words, x_scales, w1, gn, w2, offs, ea
         turn_back(1)
         west_difference(second)
         east_difference(block[2])
-        quantize_w2(1, "early_east3")
-        nc.vector.tensor_scalar(late_east[:, PACK - 2, P:], u[3][:].indirect(east_sb[:, entries(block[3])]), 0.5, 0.0, ALU.mult, ALU.add)
+        nc.vector.tensor_scalar(centre[:, 0, :], u[0][:, second], 2.0, None, ALU.mult)
         clamp_low(0, 4, block[2])
         east_difference(block[3])
         clamp_high(0, 4, block[2])

@@ -44,22 +44,20 @@ def tile_picked_minmod_none_p_kernel(tc, x_words, x_scales, w1, gn, w2, offs, ea
         xg_scales = sb.tile([P, S], U8, name="xg_scales", align_bytes=64)
 
         nc.sync.dma_start(offs_sb[:], offs)
-        nc.scalar.dma_start(gain[:], gn.rearrange("(p t) o -> p (t o)", t=PACK))
-        nc.sync.dma_start(xs[0:32, :].bitcast(I32), x_scales[0].bitcast(I32).unsqueeze(1).to_broadcast([16, 2, T // 4]))
-        nc.vector.memset(xs[32:64, :].bitcast(I32), 0)
-        nc.vector.memset(xs[64:128, :].bitcast(I32), 0)
+        nc.sync.dma_start(xs[112:128, :].bitcast(I32), x_scales[0].bitcast(I32))
+        nc.vector.memset(xs[0:96, :].bitcast(I32), 0)
+        nc.vector.memset(xs[96:112, :].bitcast(I32), 0)
         nc.vector.memset(xg_scales[:].bitcast(I32), 0)
         nc.sync.dma_start(w1_raw[:], w1.rearrange("(p j) c -> p j c", j=PACK))
         nc.sync.dma_start(east_sb[:], east)
         nc.sync.dma_start(xw[:].bitcast(I32), x_words[0].rearrange("p n t -> p (n t)").bitcast(I32))
         nc.sync.dma_start(west_sb[:], west)
+        nc.sync.dma_start(gain[:], gn.rearrange("(p t) o -> p (t o)", t=PACK))
         make_identity(nc, ident[:])
-        nc.vector.tensor_scalar(g_pos[:], gain[:, 0:1], 0.5, None, ALU.mult)
-        nc.vector.tensor_scalar(g_neg[:], gain[:, 0:1], -0.5, None, ALU.mult)
 
         nc.vector.tensor_copy(spread_scales[:], xs[:].indirect(offs_sb[:]))
         for q in range(4):
-            nc.sync.dma_start(xg_scales[32 * q : 32 * q + 4, :].bitcast(I32), spread_scales[8 * q : 8 * q + 8 : 2, :].bitcast(I32))
+            nc.sync.dma_start(xg_scales[32 * q : 32 * q + 4, :].bitcast(I32), spread_scales[112 + 4 * q : 116 + 4 * q, :].bitcast(I32))
 
         w2_raw = [shared.tile([P, PACK, HALF], F32, name=f"w2_raw{h}", offset=h * W2_HALF_BYTES, align_bytes=64) for h in range(2)]
         for h in range(2):
@@ -77,6 +75,9 @@ def tile_picked_minmod_none_p_kernel(tc, x_words, x_scales, w1, gn, w2, offs, ea
             scales=w1_scales[:].rearrange("p t m -> p (t m)"),
             in_=w1_bf[:],
         )
+
+        nc.scalar.activation(g_pos[:], gain[:, 0:1], COPY, scale=0.5)
+        nc.scalar.activation(g_neg[:], gain[:, 0:1], COPY, scale=-0.5)
 
         xg = sb.tile([P, S], U32, name="xg", align_bytes=64)
         for h in range(2):
@@ -132,6 +133,7 @@ def tile_picked_minmod_none_p_kernel(tc, x_words, x_scales, w1, gn, w2, offs, ea
         a = {0: sb.tile([P, PACK, HALF], F32, name="a0", align_bytes=64)}
         b = {h: sb.tile([P, PACK, HALF], F32, name=f"b{h}", align_bytes=64) for h in range(2)}
         low = sb.tile([P, PACK, S], F32, name="low", align_bytes=64)
+        last_low = sb.tile([P, 1, HALF], F32, name="last_low", tag="last_low", align_bytes=64)
         slope = sb.tile([P, PACK, S], F32, name="slope", align_bytes=64)
         early_west = {}
         early_east = {}
@@ -177,13 +179,16 @@ def tile_picked_minmod_none_p_kernel(tc, x_words, x_scales, w1, gn, w2, offs, ea
         def east_difference(cells):
             nc.vector.scalar_tensor_tensor(b[1][:, 1:, local(cells)], centre[:, 1:, local(cells)], -0.5, late_east[:, :, local(cells)], ALU.mult, ALU.add)
 
+        def low_of(t0, t1, cells):
+            return last_low[:] if t0 == PACK - 1 else low[:, t0:t1, cells]
+
         def clamp_low(t0, t1, cells):
             h, c = half(cells), local(cells)
-            nc.vector.scalar_tensor_tensor(low[:, t0:t1, cells], b[h][:, t0:t1, c], 0.0, a[h][:, t0:t1, c], ALU.min, ALU.max)
+            nc.vector.scalar_tensor_tensor(low_of(t0, t1, cells), b[h][:, t0:t1, c], 0.0, a[h][:, t0:t1, c], ALU.min, ALU.max)
 
         def clamp_high(t0, t1, cells):
             h, c = half(cells), local(cells)
-            nc.vector.scalar_tensor_tensor(slope[:, t0:t1, cells], b[h][:, t0:t1, c], 0.0, low[:, t0:t1, cells], ALU.max, ALU.min)
+            nc.vector.scalar_tensor_tensor(slope[:, t0:t1, cells], b[h][:, t0:t1, c], 0.0, low_of(t0, t1, cells), ALU.max, ALU.min)
 
         z_bf = {}
         z_codes = {}
@@ -263,8 +268,8 @@ def tile_picked_minmod_none_p_kernel(tc, x_words, x_scales, w1, gn, w2, offs, ea
         block = [slice(r * P, (r + 1) * P) for r in range(4)]
 
         leave(2)
-        fused_east(first)
         nc.vector.tensor_scalar(v0[:, second], u[0][:, second], -1.0, None, ALU.mult)
+        fused_east(first)
         fused_east(second)
         fused_west(first)
         quantize_w2(0, "w2_scales0")
@@ -287,14 +292,18 @@ def tile_picked_minmod_none_p_kernel(tc, x_words, x_scales, w1, gn, w2, offs, ea
         clamp_high(0, 2, first)
         add_slope(0, 0, 2)
         add_slope(1, 0, 2)
+        clamp_low(2, 3, first)
         differences(3)
+        clamp_high(2, 3, first)
+        add_slope(0, 2, 3)
+        add_slope(1, 2, 3)
+        clamp_low(3, 4, first)
         quantize_w2(1, "early_west3")
-        clamp_low(2, 4, first)
-        a[1] = sb.tile([P, PACK, HALF], F32, name="a1", tag="early_east1", align_bytes=64)
+        clamp_high(3, 4, first)
+        add_slope(0, 3, 4)
+        add_slope(1, 3, 4)
+        a[1] = sb.tile([P, PACK, HALF], F32, name="a1", tag="last_low", align_bytes=64)
         fused_west(second)
-        clamp_high(2, 4, first)
-        add_slope(0, 2, 4)
-        add_slope(1, 2, 4)
         round_sum(0)
         round_sum(1)
         turn_back(0)

@@ -44,7 +44,7 @@ def tile_picked_minmod_none_p_kernel(tc, x_words, x_scales, w1, gn, w2, offs, ea
         xg_scales = sb.tile([P, S], U8, name="xg_scales", align_bytes=64)
 
         nc.sync.dma_start(offs_sb[:], offs)
-        nc.sync.dma_start(xs[112:128, :].bitcast(I32), x_scales[0].bitcast(I32))
+        nc.scalar.dma_start(xs[112:128, :].bitcast(I32), x_scales[0].bitcast(I32))
         nc.vector.memset(xs[0:96, :].bitcast(I32), 0)
         nc.vector.memset(xs[96:112, :].bitcast(I32), 0)
         nc.vector.memset(xg_scales[:].bitcast(I32), 0)

@@ -45,6 +45,7 @@ def tile_picked_minmod_none_p_kernel(tc, x_words, x_scales, w1, gn, w2, offs, ea
 
         nc.sync.dma_start(offs_sb[:], offs)
         nc.scalar.dma_start(xs[112:128, :].bitcast(I32), x_scales[0].bitcast(I32))
+        nc.scalar.dma_start(gain[:], gn.rearrange("(p t) o -> p (t o)", t=PACK))
         nc.vector.memset(xs[0:96, :].bitcast(I32), 0)
         nc.vector.memset(xs[96:112, :].bitcast(I32), 0)
         nc.vector.memset(xg_scales[:].bitcast(I32), 0)
@@ -52,7 +53,6 @@ def tile_picked_minmod_none_p_kernel(tc, x_words, x_scales, w1, gn, w2, offs, ea
         nc.sync.dma_start(east_sb[:], east)
         nc.sync.dma_start(xw[:].bitcast(I32), x_words[0].rearrange("p n t -> p (n t)").bitcast(I32))
         nc.sync.dma_start(west_sb[:], west)
-        nc.sync.dma_start(gain[:], gn.rearrange("(p t) o -> p (t o)", t=PACK))
         make_identity(nc, ident[:])
 
         nc.vector.tensor_copy(spread_scales[:], xs[:].indirect(offs_sb[:]))

@@ -50,8 +50,8 @@ def tile_picked_minmod_none_p_kernel(tc, x_words, x_scales, w1, gn, w2, offs, ea
         nc.vector.memset(xs[96:112, :].bitcast(I32), 0)
         nc.vector.memset(xg_scales[:].bitcast(I32), 0)
         nc.sync.dma_start(w1_raw[:], w1.rearrange("(p j) c -> p j c", j=PACK))
-        nc.sync.dma_start(east_sb[:], east)
         nc.sync.dma_start(xw[:].bitcast(I32), x_words[0].rearrange("p n t -> p (n t)").bitcast(I32))
+        nc.sync.dma_start(east_sb[:], east)
         nc.sync.dma_start(west_sb[:], west)
         make_identity(nc, ident[:])
 

@@ -70,11 +70,24 @@ def tile_picked_minmod_none_p_kernel(tc, x_words, x_scales, w1, gn, w2, offs, ea
         w1_src = w1_raw[:].rearrange("p j (m t) -> p m t j", t=PACK)
         nc.vector.tensor_copy(w1_dst[:, :W1_VECTOR], w1_src[:, :W1_VECTOR])
         nc.scalar.copy(w1_dst[:, W1_VECTOR:], w1_src[:, W1_VECTOR:])
-        nc.vector.quantize_mx(
-            out=w1_codes[:].rearrange("p t m -> p (t m)").bitcast(FP8X4),
-            scales=w1_scales[:].rearrange("p t m -> p (t m)"),
-            in_=w1_bf[:],
-        )
+        for pair in range(2):
+            planes = slice(2 * pair, 2 * pair + 2)
+            nc.vector.quantize_mx(
+                out=w1_codes[:, planes, :].rearrange("p t m -> p (t m)").bitcast(FP8X4),
+                scales=w1_scales[:, planes, :].rearrange("p t m -> p (t m)"),
+                in_=w1_bf[:, pair * 2 * H : (pair + 1) * 2 * H],
+            )
+        warm = psum.tile([P, HALF], F32, name="warm", tag="bank6")
+        for i in range(4):
+            nc.tensor.matmul_mx(
+                out=warm[:],
+                lhsT=w1_codes[:, i % 2, :].bitcast(FP8X4),
+                lhsT_scale=w1_scales[:, i % 2, :],
+                rhs=w1_codes[:, :2, :].rearrange("p t m -> p (t m)").bitcast(FP8X4),
+                rhs_scale=w1_scales[:, :2, :].rearrange("p t m -> p (t m)"),
+                start=True,
+                stop=True,
+            )
 
         nc.scalar.activation(g_pos[:], gain[:, 0:1], COPY, scale=0.5)
         nc.scalar.activation(g_neg[:], gain[:, 0:1], COPY, scale=-0.5)

@@ -77,17 +77,6 @@ def tile_picked_minmod_none_p_kernel(tc, x_words, x_scales, w1, gn, w2, offs, ea
                 scales=w1_scales[:, planes, :].rearrange("p t m -> p (t m)"),
                 in_=w1_bf[:, pair * 2 * H : (pair + 1) * 2 * H],
             )
-        warm = psum.tile([P, HALF], F32, name="warm", tag="bank6")
-        for i in range(4):
-            nc.tensor.matmul_mx(
-                out=warm[:],
-                lhsT=w1_codes[:, i % 2, :].bitcast(FP8X4),
-                lhsT_scale=w1_scales[:, i % 2, :],
-                rhs=w1_codes[:, :2, :].rearrange("p t m -> p (t m)").bitcast(FP8X4),
-                rhs_scale=w1_scales[:, :2, :].rearrange("p t m -> p (t m)"),
-                start=True,
-                stop=True,
-            )
 
         nc.scalar.activation(g_pos[:], gain[:, 0:1], COPY, scale=0.5)
         nc.scalar.activation(g_neg[:], gain[:, 0:1], COPY, scale=-0.5)

@@ -82,8 +82,9 @@ def tile_picked_minmod_none_p_kernel(tc, x_words, x_scales, w1, gn, w2, offs, ea
         nc.scalar.activation(g_neg[:], gain[:, 0:1], COPY, scale=-0.5)
 
         xg = sb.tile([P, S], U32, name="xg", align_bytes=64)
-        for h in range(2):
-            nc.vector.tensor_copy(xg[:, h * HALF : (h + 1) * HALF], xw[:].indirect(offs_sb[:, 16 * h : 16 * h + 16]))
+        pieces = [slice(0, HALF), slice(HALF, HALF + P), slice(HALF + P, S)]
+        for cols in pieces:
+            nc.vector.tensor_copy(xg[:, cols], xw[:].indirect(offs_sb[:, cols.start // 16 : cols.stop // 16]))
 
         u = [sb.tile([P, S], F32, name=f"u{t}", align_bytes=64) for t in range(PACK)]
 
@@ -116,16 +117,17 @@ def tile_picked_minmod_none_p_kernel(tc, x_words, x_scales, w1, gn, w2, offs, ea
         round_w2(0, "w2_bf0")
         v0 = shared.tile([P, S], F32, name="v0", offset=0, align_bytes=64)
 
-        for h in range(2):
-            acc = psum.tile([P, HALF], F32, name=f"y0{h}", tag=f"bank{h}")
-            cols = slice(h * HALF, (h + 1) * HALF)
+        for i, cols in enumerate(pieces):
+            acc = psum.tile([P, cols.stop - cols.start], F32, name=f"y0{i}", tag=f"bank{(0, 1, 6)[i]}")
             first_product(acc[:], 0, cols)
             nc.scalar.activation(u[0][:, cols], acc[:], COPY, scale=g_pos[:])
-            if h == 0:
+            if i == 0:
                 nc.vector.tensor_scalar(v0[:, cols], acc[:], g_neg[:], None, ALU.mult)
-            acc = psum.tile([P, HALF], F32, name=f"y1{h}", tag=f"bank{(2, 7)[h]}")
-            first_product(acc[:], 1, cols)
-            nc.scalar.activation(u[1][:, cols], acc[:], COPY, scale=gain[:, 1:2])
+            if i != 1:
+                cols = slice(i // 2 * HALF, (i // 2 + 1) * HALF)
+                acc = psum.tile([P, HALF], F32, name=f"y1{i}", tag=f"bank{(2, 7)[i // 2]}")
+                first_product(acc[:], 1, cols)
+                nc.scalar.activation(u[1][:, cols], acc[:], COPY, scale=gain[:, 1:2])
 
         def leave(t):
             acc = psum.tile([P, S], F32, name=f"y{t}", tag=f"bank{t + 1}")

@@ -134,7 +134,7 @@ def tile_picked_minmod_none_p_kernel(tc, x_words, x_scales, w1, gn, w2, offs, ea
             first_product(acc[:], t, slice(0, S))
             nc.scalar.activation(u[t][:], acc[:], COPY, scale=gain[:, t : t + 1])
 
-        a = {0: sb.tile([P, PACK, HALF], F32, name="a0", align_bytes=64)}
+        a = {0: sb.tile([P, PACK, HALF], F32, name="a0", tag="a0", align_bytes=64)}
         b = {h: sb.tile([P, PACK, HALF], F32, name=f"b{h}", align_bytes=64) for h in range(2)}
         low = sb.tile([P, PACK, S], F32, name="low", align_bytes=64)
         last_low = sb.tile([P, 1, HALF], F32, name="last_low", tag="last_low", align_bytes=64)
@@ -184,7 +184,7 @@ def tile_picked_minmod_none_p_kernel(tc, x_words, x_scales, w1, gn, w2, offs, ea
             nc.vector.scalar_tensor_tensor(b[1][:, 1:, local(cells)], centre[:, 1:, local(cells)], -0.5, late_east[:, :, local(cells)], ALU.mult, ALU.add)
 
         def low_of(t0, t1, cells):
-            return last_low[:] if t0 == PACK - 1 else low[:, t0:t1, cells]
+            return last_low[:, :, cells] if t0 == PACK - 1 else low[:, t0:t1, cells]
 
         def clamp_low(t0, t1, cells):
             h, c = half(cells), local(cells)
@@ -301,11 +301,13 @@ def tile_picked_minmod_none_p_kernel(tc, x_words, x_scales, w1, gn, w2, offs, ea
         clamp_high(2, 3, first)
         add_slope(0, 2, 3)
         add_slope(1, 2, 3)
-        clamp_low(3, 4, first)
-        quantize_w2(1, "early_west3")
-        clamp_high(3, 4, first)
+        clamp_low(3, 4, block[0])
+        clamp_low(3, 4, block[1])
+        clamp_high(3, 4, block[0])
         add_slope(0, 3, 4)
+        clamp_high(3, 4, block[1])
         add_slope(1, 3, 4)
+        quantize_w2(1, "a0")
         a[1] = sb.tile([P, PACK, HALF], F32, name="a1", tag="last_low", align_bytes=64)
         fused_west(second)
         round_sum(0)
@@ -318,14 +320,14 @@ def tile_picked_minmod_none_p_kernel(tc, x_words, x_scales, w1, gn, w2, offs, ea
         clamp_low(0, 4, block[2])
         east_difference(block[3])
         clamp_high(0, 4, block[2])
-        clamp_low(0, 4, block[3])
         quantize_z(block[0])
         second_product(block[0], 0, 2, 1, nc.scalar.copy)
         second_product(block[0], 2, 4, 2, nc.scalar.copy)
-        add_centre(block[2], 1)
+        clamp_low(0, 4, block[3])
         quantize_z(block[1])
         second_product(block[1], 0, 2, 7, nc.scalar.copy)
         second_product(block[1], 2, 4, 3, nc.scalar.copy)
+        add_centre(block[2], 1)
         clamp_high(0, 4, block[3])
         quantize_z(block[2])
         second_product(block[2], 0, 2, 5, nc.scalar.copy)

@@ -142,7 +142,8 @@ def tile_picked_minmod_none_p_kernel(tc, x_words, x_scales, w1, gn, w2, offs, ea
         early_west = {}
         early_east = {}
         late_west = sb.tile([P, PACK - 1, HALF], F32, name="late_west", align_bytes=64)
-        late_east = sb.tile([P, PACK - 1, HALF], F32, name="late_east", align_bytes=64)
+        late_east = {HALF: sb.tile([P, PACK - 1, P], F32, name="late_east2", align_bytes=64)}
+        last_slope = sb.tile([P, 1, P], F32, name="last_slope", tag="last_slope", align_bytes=64)
 
         def entries(cells):
             return slice(cells.start // 16, cells.stop // 16)
@@ -171,7 +172,7 @@ def tile_picked_minmod_none_p_kernel(tc, x_words, x_scales, w1, gn, w2, offs, ea
 
         def east_gathers(cells, t1):
             for t in range(1, t1):
-                nc.scalar.activation(late_east[:, t - 1, local(cells)], u[t][:].indirect(east_sb[:, entries(cells)]), COPY, scale=0.5)
+                nc.scalar.activation(late_east[cells.start][:, t - 1, :], u[t][:].indirect(east_sb[:, entries(cells)]), COPY, scale=0.5)
 
         def differences(t):
             nc.vector.scalar_tensor_tensor(a[0][:, t, :], u[t][:, first], 0.5, early_west[t][:], ALU.mult, ALU.add)
@@ -181,7 +182,7 @@ def tile_picked_minmod_none_p_kernel(tc, x_words, x_scales, w1, gn, w2, offs, ea
             nc.vector.scalar_tensor_tensor(a[1][:, 1:, local(cells)], centre[:, 1:, local(cells)], 0.5, late_west[:, :, local(cells)], ALU.mult, ALU.add)
 
         def east_difference(cells):
-            nc.vector.scalar_tensor_tensor(b[1][:, 1:, local(cells)], centre[:, 1:, local(cells)], -0.5, late_east[:, :, local(cells)], ALU.mult, ALU.add)
+            nc.vector.scalar_tensor_tensor(b[1][:, 1:, local(cells)], centre[:, 1:, local(cells)], -0.5, late_east[cells.start][:], ALU.mult, ALU.add)
 
         def low_of(t0, t1, cells):
             return last_low[:, :, cells] if t0 == PACK - 1 else low[:, t0:t1, cells]
@@ -190,9 +191,12 @@ def tile_picked_minmod_none_p_kernel(tc, x_words, x_scales, w1, gn, w2, offs, ea
             h, c = half(cells), local(cells)
             nc.vector.scalar_tensor_tensor(low_of(t0, t1, cells), b[h][:, t0:t1, c], 0.0, a[h][:, t0:t1, c], ALU.min, ALU.max)
 
+        def slope_of(t0, t1, cells):
+            return last_slope[:] if t0 == PACK - 1 and cells == block[0] else slope[:, t0:t1, cells]
+
         def clamp_high(t0, t1, cells):
             h, c = half(cells), local(cells)
-            nc.vector.scalar_tensor_tensor(slope[:, t0:t1, cells], b[h][:, t0:t1, c], 0.0, low_of(t0, t1, cells), ALU.max, ALU.min)
+            nc.vector.scalar_tensor_tensor(slope_of(t0, t1, cells), b[h][:, t0:t1, c], 0.0, low_of(t0, t1, cells), ALU.max, ALU.min)
 
         z_bf = {}
         z_codes = {}
@@ -220,7 +224,7 @@ def tile_picked_minmod_none_p_kernel(tc, x_words, x_scales, w1, gn, w2, offs, ea
 
         def add_slope(r, t0, t1):
             for t in range(t0, t1):
-                nc.tensor.matmul(zt[r][:, t, :], slope[:, t, r * P : (r + 1) * P], ident[:], start=False, stop=(t == PACK - 1), is_transpose=True)
+                nc.tensor.matmul(zt[r][:, t, :], slope_of(t, t + 1, block[r])[:, 0, :], ident[:], start=False, stop=(t == PACK - 1), is_transpose=True)
 
         pairs = {}
 
@@ -283,7 +287,6 @@ def tile_picked_minmod_none_p_kernel(tc, x_words, x_scales, w1, gn, w2, offs, ea
         early_gathers(3)
         west_gathers(second)
         east_gathers(block[2], PACK)
-        east_gathers(block[3], PACK)
         open_sum(0)
         open_sum(1)
         differences(1)
@@ -310,24 +313,27 @@ def tile_picked_minmod_none_p_kernel(tc, x_words, x_scales, w1, gn, w2, offs, ea
         quantize_w2(1, "a0")
         a[1] = sb.tile([P, PACK, HALF], F32, name="a1", tag="last_low", align_bytes=64)
         fused_west(second)
+        late_east[block[3].start] = sb.tile([P, PACK - 1, P], F32, name="late_east3", tag="last_slope", align_bytes=64)
         round_sum(0)
+        east_gathers(block[3], PACK)
         round_sum(1)
         turn_back(0)
         turn_back(1)
-        west_difference(second)
+        west_difference(block[2])
         east_difference(block[2])
+        west_difference(block[3])
         nc.vector.tensor_scalar(centre[:, 0, :], u[0][:, second], 2.0, None, ALU.mult)
         clamp_low(0, 4, block[2])
         east_difference(block[3])
         clamp_high(0, 4, block[2])
+        clamp_low(0, 4, block[3])
         quantize_z(block[0])
         second_product(block[0], 0, 2, 1, nc.scalar.copy)
         second_product(block[0], 2, 4, 2, nc.scalar.copy)
-        clamp_low(0, 4, block[3])
+        add_centre(block[2], 1)
         quantize_z(block[1])
         second_product(block[1], 0, 2, 7, nc.scalar.copy)
         second_product(block[1], 2, 4, 3, nc.scalar.copy)
-        add_centre(block[2], 1)
         clamp_high(0, 4, block[3])
         quantize_z(block[2])
         second_product(block[2], 0, 2, 5, nc.scalar.copy)

@@ -326,10 +326,10 @@ def tile_picked_minmod_none_p_kernel(tc, x_words, x_scales, w1, gn, w2, offs, ea
         clamp_low(0, 4, block[2])
         east_difference(block[3])
         clamp_high(0, 4, block[2])
-        clamp_low(0, 4, block[3])
         quantize_z(block[0])
         second_product(block[0], 0, 2, 1, nc.scalar.copy)
         second_product(block[0], 2, 4, 2, nc.scalar.copy)
+        clamp_low(0, 4, block[3])
         add_centre(block[2], 1)
         quantize_z(block[1])
         second_product(block[1], 0, 2, 7, nc.scalar.copy)

from contextlib import ExitStack

import concourse.mybir as mybir
from concourse.masks import make_identity

K, T, S, N, H = 512, 2048, 512, 512, 512
FLOPS = 2 * K * H * S + 2 * H * N * S

F32 = mybir.dt.float32
BF16 = mybir.dt.bfloat16
I32 = mybir.dt.int32
U32 = mybir.dt.uint32
U16 = mybir.dt.uint16
U8 = mybir.dt.uint8
FP8X4 = mybir.dt.float8_e4m3fn_x4
ALU = mybir.AluOpType
COPY = mybir.ActivationFunctionType.Copy

P = 128
PACK = 4
HALF = S // 2
W1_VECTOR = 84
W2_HALF_BYTES = 4 * PACK * HALF


def tile_picked_minmod_none_p_kernel(tc, x_words, x_scales, w1, gn, w2, offs, east, west, out):
    nc = tc.nc
    with ExitStack() as ctx:
        sb = ctx.enter_context(tc.tile_pool(name="sb", bufs=1))
        shared = ctx.enter_context(tc.tile_pool(name="shared", bufs=1))
        psum = ctx.enter_context(tc.psum_pool(name="psum", bufs=1))

        offs_sb = sb.tile([P, S // 16], U16, name="offs_sb")
        east_sb = sb.tile([P, S // 16], U16, name="east_sb")
        west_sb = sb.tile([P, S // 16], U16, name="west_sb")
        xs = shared.tile([P, T], U8, name="xs", offset=W2_HALF_BYTES - T // 2, align_bytes=64)
        xw = sb.tile([P, T], U32, name="xw", align_bytes=64)
        w1_raw = sb.tile([P, PACK, H], F32, name="w1_raw", align_bytes=64)
        gain = sb.tile([P, PACK], F32, name="gain")
        g_pos = sb.tile([P, 1], F32, name="g_pos")
        g_neg = sb.tile([P, 1], F32, name="g_neg")
        ident = sb.tile([P, P], F32, name="ident", align_bytes=64)
        spread_scales = sb.tile([P, S], U8, name="spread_scales", align_bytes=64)
        xg_scales = sb.tile([P, S], U8, name="xg_scales", align_bytes=64)

        nc.sync.dma_start(offs_sb[:], offs)
        nc.scalar.dma_start(xs[112:128, :].bitcast(I32), x_scales[0].bitcast(I32))
        nc.scalar.dma_start(gain[:], gn.rearrange("(p t) o -> p (t o)", t=PACK))
        nc.vector.memset(xs[0:96, :].bitcast(I32), 0)
        nc.vector.memset(xs[96:112, :].bitcast(I32), 0)
        nc.vector.memset(xg_scales[:].bitcast(I32), 0)
        nc.sync.dma_start(w1_raw[:], w1.rearrange("(p j) c -> p j c", j=PACK))
        nc.sync.dma_start(xw[:].bitcast(I32), x_words[0].rearrange("p n t -> p (n t)").bitcast(I32))
        nc.sync.dma_start(east_sb[:], east)
        nc.sync.dma_start(west_sb[:], west)
        make_identity(nc, ident[:])

        nc.vector.tensor_copy(spread_scales[:], xs[:].indirect(offs_sb[:]))
        for q in range(4):
            nc.sync.dma_start(xg_scales[32 * q : 32 * q + 4, :].bitcast(I32), spread_scales[112 + 4 * q : 116 + 4 * q, :].bitcast(I32))

        w2_raw = [shared.tile([P, PACK, HALF], F32, name=f"w2_raw{h}", offset=h * W2_HALF_BYTES, align_bytes=64) for h in range(2)]
        for h in range(2):
            nc.sync.dma_start(w2_raw[h][:], w2[:, h * HALF : (h + 1) * HALF].rearrange("(p j) c -> p j c", j=PACK))

        w1_bf = sb.tile([P, PACK * H], BF16, name="w1_bf", align_bytes=64)
        w1_codes = sb.tile([P, PACK, P], U32, name="w1_codes", align_bytes=64)
        w1_scales = sb.tile([P, PACK, P], U8, name="w1_scales", align_bytes=64)
        w1_dst = w1_bf[:].rearrange("p (t m j) -> p m t j", t=PACK, j=PACK)
        w1_src = w1_raw[:].rearrange("p j (m t) -> p m t j", t=PACK)
        nc.vector.tensor_copy(w1_dst[:, :W1_VECTOR], w1_src[:, :W1_VECTOR])
        nc.scalar.copy(w1_dst[:, W1_VECTOR:], w1_src[:, W1_VECTOR:])
        for pair in range(2):
            planes = slice(2 * pair, 2 * pair + 2)
            nc.vector.quantize_mx(
                out=w1_codes[:, planes, :].rearrange("p t m -> p (t m)").bitcast(FP8X4),
                scales=w1_scales[:, planes, :].rearrange("p t m -> p (t m)"),
                in_=w1_bf[:, pair * 2 * H : (pair + 1) * 2 * H],
            )

        nc.scalar.activation(g_pos[:], gain[:, 0:1], COPY, scale=0.5)
        nc.scalar.activation(g_neg[:], gain[:, 0:1], COPY, scale=-0.5)

        xg = sb.tile([P, S], U32, name="xg", align_bytes=64)
        pieces = [slice(0, HALF), slice(HALF, HALF + P), slice(HALF + P, S)]
        for cols in pieces:
            nc.vector.tensor_copy(xg[:, cols], xw[:].indirect(offs_sb[:, cols.start // 16 : cols.stop // 16]))

        u = [sb.tile([P, S], F32, name=f"u{t}", align_bytes=64) for t in range(PACK)]

        def first_product(acc, t, cols):
            nc.tensor.matmul_mx(
                out=acc,
                lhsT=w1_codes[:, t, :].bitcast(FP8X4),
                lhsT_scale=w1_scales[:, t, :],
                rhs=xg[:, cols].bitcast(FP8X4),
                rhs_scale=xg_scales[:, cols],
                start=True,
                stop=True,
            )

        w2_bf = {}
        w2_codes = sb.tile([P, N], U32, name="w2_codes", align_bytes=64)
        w2_scales = {}

        def round_w2(h, tag):
            w2_bf[h] = sb.tile([P, PACK * HALF], BF16, name=f"w2_bf{h}", tag=tag, align_bytes=64)
            nc.vector.tensor_copy(
                w2_bf[h][:].rearrange("p (c i j) -> p c j i", i=4, j=PACK),
                w2_raw[h][:].rearrange("p j (c i) -> p c j i", i=4),
            )

        def quantize_w2(h, tag):
            w2_scales[h] = sb.tile([P, HALF], U8, name=f"w2_scales{h}", tag=tag, align_bytes=64)
            nc.vector.quantize_mx(out=w2_codes[:, h * HALF : (h + 1) * HALF].bitcast(FP8X4), scales=w2_scales[h][:], in_=w2_bf[h][:])

        round_w2(0, "w2_bf0")
        v0 = shared.tile([P, S], F32, name="v0", offset=0, align_bytes=64)

        for i, cols in enumerate(pieces):
            acc = psum.tile([P, cols.stop - cols.start], F32, name=f"y0{i}", tag=f"bank{(0, 1, 6)[i]}")
            first_product(acc[:], 0, cols)
            nc.scalar.activation(u[0][:, cols], acc[:], COPY, scale=g_pos[:])
            if i == 0:
                nc.vector.tensor_scalar(v0[:, cols], acc[:], g_neg[:], None, ALU.mult)
            if i != 1:
                cols = slice(i // 2 * HALF, (i // 2 + 1) * HALF)
                acc = psum.tile([P, HALF], F32, name=f"y1{i}", tag=f"bank{(2, 7)[i // 2]}")
                first_product(acc[:], 1, cols)
                nc.scalar.activation(u[1][:, cols], acc[:], COPY, scale=gain[:, 1:2])

        def leave(t):
            acc = psum.tile([P, S], F32, name=f"y{t}", tag=f"bank{t + 1}")
            first_product(acc[:], t, slice(0, S))
            nc.scalar.activation(u[t][:], acc[:], COPY, scale=gain[:, t : t + 1])

        a = {0: sb.tile([P, PACK, HALF], F32, name="a0", tag="a0", align_bytes=64)}
        b = {h: sb.tile([P, PACK, HALF], F32, name=f"b{h}", align_bytes=64) for h in range(2)}
        low = sb.tile([P, PACK, S], F32, name="low", align_bytes=64)
        last_low = sb.tile([P, 1, HALF], F32, name="last_low", tag="last_low", align_bytes=64)
        slope = sb.tile([P, PACK, S], F32, name="slope", align_bytes=64)
        early_west = {}
        early_east = {}
        late_west = sb.tile([P, PACK - 1, HALF], F32, name="late_west", align_bytes=64)
        late_east = {HALF: sb.tile([P, PACK - 1, P], F32, name="late_east2", align_bytes=64)}
        last_slope = sb.tile([P, 1, P], F32, name="last_slope", tag="last_slope", align_bytes=64)

        def entries(cells):
            return slice(cells.start // 16, cells.stop // 16)

        def half(cells):
            return cells.start // HALF

        def local(cells):
            return slice(cells.start % HALF, (cells.stop - 1) % HALF + 1)

        def fused_east(cells):
            nc.vector.tensor_tensor(b[half(cells)][:, 0, :], u[0][:].indirect(east_sb[:, entries(cells)]), v0[:, cells], ALU.add)

        def fused_west(cells):
            nc.vector.tensor_tensor(a[half(cells)][:, 0, :], v0[:].indirect(west_sb[:, entries(cells)]), u[0][:, cells], ALU.add)

        def early_gathers(t):
            early_west[t] = sb.tile([P, HALF], F32, name=f"early_west{t}", tag=f"early_west{t}", align_bytes=64)
            early_east[t] = sb.tile([P, HALF], F32, name=f"early_east{t}", tag=f"early_east{t}", align_bytes=64)
            nc.scalar.activation(early_west[t][:], u[t][:].indirect(west_sb[:, entries(first)]), COPY, scale=-0.5)
            nc.scalar.activation(early_east[t][:], u[t][:].indirect(east_sb[:, entries(first)]), COPY, scale=0.5)

        def west_gathers(cells):
            for t in range(1, PACK):
                nc.scalar.activation(late_west[:, t - 1, local(cells)], u[t][:].indirect(west_sb[:, entries(cells)]), COPY, scale=-0.5)

        def east_gathers(cells, t1):
            for t in range(1, t1):
                nc.scalar.activation(late_east[cells.start][:, t - 1, :], u[t][:].indirect(east_sb[:, entries(cells)]), COPY, scale=0.5)

        def differences(t):
            nc.vector.scalar_tensor_tensor(a[0][:, t, :], u[t][:, first], 0.5, early_west[t][:], ALU.mult, ALU.add)
            nc.vector.scalar_tensor_tensor(b[0][:, t, :], u[t][:, first], -0.5, early_east[t][:], ALU.mult, ALU.add)

        def west_difference(cells):
            nc.vector.scalar_tensor_tensor(a[1][:, 1:, local(cells)], centre[:, 1:, local(cells)], 0.5, late_west[:, :, local(cells)], ALU.mult, ALU.add)

        def east_difference(cells):
            nc.vector.scalar_tensor_tensor(b[1][:, 1:, local(cells)], centre[:, 1:, local(cells)], -0.5, late_east[cells.start][:], ALU.mult, ALU.add)

        def low_of(t0, t1, cells):
            return last_low[:, :, cells] if t0 == PACK - 1 else low[:, t0:t1, cells]

        def clamp_low(t0, t1, cells):
            h, c = half(cells), local(cells)
            nc.vector.scalar_tensor_tensor(low_of(t0, t1, cells), b[h][:, t0:t1, c], 0.0, a[h][:, t0:t1, c], ALU.min, ALU.max)

        def slope_of(t0, t1, cells):
            return last_slope[:] if t0 == PACK - 1 and cells == block[0] else slope[:, t0:t1, cells]

        def clamp_high(t0, t1, cells):
            h, c = half(cells), local(cells)
            nc.vector.scalar_tensor_tensor(slope_of(t0, t1, cells), b[h][:, t0:t1, c], 0.0, low_of(t0, t1, cells), ALU.max, ALU.min)

        z_bf = {}
        z_codes = {}
        z_scales = {}

        def add_centre(cells, parts):
            width = (cells.stop - cells.start) // parts
            z_bf[cells.start] = sb.tile([P, parts, PACK * width], BF16, name=f"z_bf{cells.start}", align_bytes=64)
            for part in range(parts):
                some = slice(cells.start + part * width, cells.start + (part + 1) * width)
                nc.vector.tensor_tensor(
                    z_bf[cells.start][:, part, :].rearrange("p (c i t) -> p c t i", i=2, t=PACK),
                    slope[:, :, some].rearrange("p t (c i) -> p c t i", i=2),
                    centre[:, :, local(some)].rearrange("p t (c i) -> p c t i", i=2),
                    ALU.add,
                )

        zt = {}

        def open_sum(r):
            zt[r] = psum.tile([P, PACK, P], F32, name=f"zt{r}", tag=f"bank{5 + r}")
            terms = [0, 0, 1, 2, 3]
            for i, t in enumerate(terms):
                nc.tensor.matmul(zt[r][:, t, :], u[t][:, r * P : (r + 1) * P], ident[:], start=(i == 0), stop=False, is_transpose=True)

        def add_slope(r, t0, t1):
            for t in range(t0, t1):
                nc.tensor.matmul(zt[r][:, t, :], slope_of(t, t + 1, block[r])[:, 0, :], ident[:], start=False, stop=(t == PACK - 1), is_transpose=True)

        pairs = {}

        def round_sum(r):
            rounded = sb.tile([P, PACK * P], BF16, name=f"rounded{r}", align_bytes=64)
            nc.scalar.copy(
                rounded[:].rearrange("c (e p k) -> c e p k", e=2, k=2),
                zt[r][:].rearrange("c (e k) p -> c e p k", k=2),
            )
            pairs[r] = psum.tile([P, 2, P], F32, name=f"pairs{r}", tag=f"bank{(7, 3)[r]}")
            for e in range(2):
                nc.tensor.transpose(pairs[r][:, e, :], rounded[:].bitcast(F32)[:, e * P : (e + 1) * P], ident[:])

        def turn_back(r):
            z_bf[r * P] = sb.tile([P, 1, PACK * P], BF16, name=f"z_bf{r * P}", align_bytes=64)
            nc.scalar.copy(
                z_bf[r * P][:, 0, :].bitcast(F32).rearrange("p (c e) -> p c e", e=2),
                pairs[r][:].rearrange("p e c -> p c e"),
            )

        def quantize_z(cells, parts=1):
            width = cells.stop - cells.start
            z_codes[cells.start] = sb.tile([P, width], U32, name=f"z_codes{cells.start}", align_bytes=64)
            z_scales[cells.start] = sb.tile([P, width], U8, name=f"z_scales{cells.start}", align_bytes=64)
            for part in range(parts):
                cols = slice(part * width // parts, (part + 1) * width // parts)
                nc.vector.quantize_mx(out=z_codes[cells.start][:, cols].bitcast(FP8X4), scales=z_scales[cells.start][:, cols], in_=z_bf[cells.start][:, part, :])

        def second_product(cells, g0, g1, bank, copy):
            width = cells.stop - cells.start
            acc = psum.tile([P, g1 - g0, width], F32, name=f"o{cells.start}_{g0}", tag=f"bank{bank}")
            res = sb.tile([P, g1 - g0, width], F32, name=f"res{cells.start}_{g0}", align_bytes=64)
            for g in range(g0, g1):
                rows = slice(g * P, (g + 1) * P)
                nc.tensor.matmul_mx(
                    out=acc[:, g - g0, :],
                    lhsT=w2_codes[:, rows].bitcast(FP8X4),
                    lhsT_scale=w2_scales[g // 2][:, g % 2 * P : (g % 2 + 1) * P],
                    rhs=z_codes[cells.start][:].bitcast(FP8X4),
                    rhs_scale=z_scales[cells.start][:],
                    start=True,
                    stop=True,
                )
            copy(res[:], acc[:])
            nc.sync.dma_start(out[g0 * P : g1 * P, cells].rearrange("(g p) n -> p g n", p=P), res[:])

        first = slice(0, HALF)
        second = slice(HALF, S)
        block = [slice(r * P, (r + 1) * P) for r in range(4)]

        leave(2)
        nc.vector.tensor_scalar(v0[:, second], u[0][:, second], -1.0, None, ALU.mult)
        fused_east(first)
        fused_east(second)
        fused_west(first)
        quantize_w2(0, "w2_scales0")
        early_gathers(1)
        leave(3)
        early_gathers(2)
        early_gathers(3)
        west_gathers(second)
        east_gathers(block[2], PACK)
        open_sum(0)
        open_sum(1)
        differences(1)
        round_w2(1, "early_west1")
        clamp_low(0, 2, first)
        differences(2)
        centre = sb.tile([P, PACK, HALF], F32, name="centre", tag="early_west2", align_bytes=64)
        for t in range(1, PACK):
            nc.sync.dma_start(centre[:, t, :], u[t][:, second])
        clamp_high(0, 2, first)
        add_slope(0, 0, 2)
        add_slope(1, 0, 2)
        clamp_low(2, 3, first)
        differences(3)
        clamp_high(2, 3, first)
        add_slope(0, 2, 3)
        add_slope(1, 2, 3)
        clamp_low(3, 4, block[0])
        clamp_low(3, 4, block[1])
        clamp_high(3, 4, block[0])
        add_slope(0, 3, 4)
        clamp_high(3, 4, block[1])
        add_slope(1, 3, 4)
        quantize_w2(1, "a0")
        a[1] = sb.tile([P, PACK, HALF], F32, name="a1", tag="last_low", align_bytes=64)
        fused_west(second)
        late_east[block[3].start] = sb.tile([P, PACK - 1, P], F32, name="late_east3", tag="last_slope", align_bytes=64)
        round_sum(0)
        east_gathers(block[3], PACK)
        round_sum(1)
        turn_back(0)
        turn_back(1)
        west_difference(block[2])
        east_difference(block[2])
        west_difference(block[3])
        nc.vector.tensor_scalar(centre[:, 0, :], u[0][:, second], 2.0, None, ALU.mult)
        clamp_low(0, 4, block[2])
        east_difference(block[3])
        clamp_high(0, 4, block[2])
        quantize_z(block[0])
        second_product(block[0], 0, 2, 1, nc.scalar.copy)
        second_product(block[0], 2, 4, 2, nc.scalar.copy)
        clamp_low(0, 4, block[3])
        add_centre(block[2], 1)
        quantize_z(block[1])
        second_product(block[1], 0, 2, 7, nc.scalar.copy)
        second_product(block[1], 2, 4, 3, nc.scalar.copy)
        clamp_high(0, 4, block[3])
        quantize_z(block[2])
        second_product(block[2], 0, 2, 5, nc.scalar.copy)
        second_product(block[2], 2, 4, 6, nc.scalar.copy)
        add_centre(block[3], 2)
        quantize_z(block[3], 2)
        second_product(block[3], 0, 2, 0, nc.scalar.copy)
        second_product(block[3], 2, 4, 4, nc.vector.tensor_copy)
